import numpy as np
import ml_dtypes


def mxq(x, axis, fmt="e4m3"):
    dtype, down = {"e4m3": (ml_dtypes.float8_e4m3fn, 7), "e5m2": (ml_dtypes.float8_e5m2, 14)}[fmt]
    v = np.moveaxis(np.asarray(x, np.float32).astype(ml_dtypes.bfloat16).astype(np.float64), axis, -1)
    blocks = v.reshape(v.shape[:-1] + (-1, 32))
    amax = np.abs(blocks).max(-1, keepdims=True)
    byte = np.maximum(np.where(amax > 0, np.frexp(amax)[1] - 1 + 127, 0) - down, 1)
    scale = np.exp2(byte - 127.0)
    codes = (blocks / scale).astype(np.float32).astype(dtype).astype(np.float64)
    return np.moveaxis((codes * scale).reshape(v.shape), -1, axis)


WIDE = False


def mx_kscale(k):
    if not WIDE:
        return np.ones(k)
    levels = np.array([10, -10, 5, -5, 0])
    if k % 512:
        return np.exp2(np.random.permutation(np.resize(levels, k // 32))).repeat(32)
    a = np.empty((k // 512, 16))
    for p in range(k // 512):
        a[p, :8] = np.random.permutation(np.resize(levels, 8))
        for g in range(8):
            far = levels[np.abs(levels - a[p, g]) >= 10]
            a[p, g + 8] = far[np.random.randint(len(far))]
    return np.exp2(a.ravel()).repeat(32)


def f64(x):
    return np.asarray(x).astype(np.float64)


def striped(idx):
    return np.tile(idx.reshape(-1, 16).T, (8, 1)).astype(np.uint16)


def unstriped(offs):
    return offs[:16].T.reshape(-1).astype(np.int64)


def pack_weight(w):
    k, n = w.shape
    w = f64(np.asarray(w, np.float32).astype(ml_dtypes.bfloat16)).reshape(k // 32, 32, n)
    amax = np.abs(w).max(1)
    byte = np.clip(np.where(amax > 0, np.frexp(amax)[1] - 1 + 127 - 7, 1), 1, 254)
    scaled = (w * np.exp2(127.0 - byte)[:, None, :]).reshape(k, n).astype(np.float32)
    words = np.ascontiguousarray(scaled.reshape(k // 512, 128, 4, n).transpose(0, 1, 3, 2)).astype(ml_dtypes.float8_e4m3fn).view(np.uint8)
    return words, np.ascontiguousarray(byte.astype(np.uint8).reshape(k // 512, 16, n))


def unpack_weight(words, scales):
    g, p, n, _ = words.shape
    vals = np.ascontiguousarray(words).view(ml_dtypes.float8_e4m3fn).astype(np.float64) * np.repeat(np.exp2(scales.astype(np.float64) - 127.0), 8, axis=1)[..., None]
    return vals.transpose(0, 1, 3, 2).reshape(g * 512, n)


K, T, S, N, U = 1024, 2048, 512, 128, 1024


def setup_inputs():
    n = np.random.standard_normal
    s = mx_kscale(K)[:, None]
    packed_xT = pack_weight(n((K, T)) * s)
    return {
        "x_words": packed_xT[0],
        "x_scales": packed_xT[1],
        "mean": (n((N, U))).astype(np.float32),
        "var": (np.random.uniform(0.2, 2.0, (N, U))).astype(np.float32),
        "w1": (n((K, N)) / np.sqrt(K) / s).astype(np.float32),
        "w2": (n((K, N)) / np.sqrt(K) / s).astype(np.float32),
        "offs": striped(np.random.permutation(T)[:S]),
        "track": striped(np.random.permutation(U)[:S]),
    }


def reference(x_words, x_scales, mean, var, w1, w2, offs, track):
    va = f64(var)[:, unstriped(track)]
    xq = unpack_weight(x_words, x_scales)[:, unstriped(offs)]
    rr = np.exp(mxq(f64(w2), 0, "e4m3").T @ xq)
    dd = va + rr
    gain = va / dd
    y = mxq(f64(w1), 0, "e4m3").T @ xq
    mu = f64(mean)[:, unstriped(track)]
    ee = 0.1 * ((gain * (y - mu)) ** 2)
    return va - (gain * va) + ee

@@ -1,0 +1,149 @@
+from contextlib import ExitStack
+import math
+
+import concourse.mybir as mybir
+
+K, T, S, N, U = 1024, 2048, 512, 128, 1024
+FLOPS = 2 * 2 * K * N * S
+
+F32 = mybir.dt.float32
+BF16 = mybir.dt.bfloat16
+I32 = mybir.dt.int32
+U32 = mybir.dt.uint32
+U16 = mybir.dt.uint16
+U8 = mybir.dt.uint8
+FP8X4 = mybir.dt.float8_e4m3fn_x4
+ALU = mybir.AluOpType
+ACT = mybir.ActivationFunctionType
+
+P = 128
+PACK = 4
+PASSES = 2
+HALF = S // 2
+LIST_ROWS = 16
+
+
+def tile_picked_ykal_var_p_kernel(
+    tc, x_words, x_scales, mean, var, w1, w2, offs, track, out
+):
+    nc = tc.nc
+    with ExitStack() as ctx:
+        pool = ctx.enter_context(tc.tile_pool(name="keep", bufs=1))
+        psum = ctx.enter_context(tc.psum_pool(name="psum", bufs=1))
+
+        offs_sb = pool.tile([P, S // LIST_ROWS], U16, name="offs_sb")
+        track_sb = pool.tile([P, S // LIST_ROWS], U16, name="track_sb")
+        var_sb = pool.tile([P, U], F32, name="var_sb")
+        mean_sb = pool.tile([P, U], F32, name="mean_sb")
+        words = [pool.tile([P, T], I32, name=f"words{o}") for o in range(PASSES)]
+        scales = pool.tile([P, T], U8, name="scales")
+        w1_raw = [pool.tile([P, PACK, N], F32, name=f"w1_raw{o}") for o in range(PASSES)]
+        w2_raw = [pool.tile([P, PACK, N], F32, name=f"w2_raw{o}") for o in range(PASSES)]
+
+        def load_words(o):
+            nc.sync.dma_start(words[o][:], x_words[o].rearrange("p t b -> p (t b)").bitcast(I32))
+
+        def load_scales():
+            for q in range(4):
+                nc.sync.dma_start(
+                    scales[32 * q : 32 * q + 8, :].bitcast(I32),
+                    x_scales[:, 4 * q : 4 * q + 4, :].bitcast(I32),
+                )
+
+        def load_weight(raw, w, o):
+            nc.sync.dma_start(raw[o][:], w[512 * o : 512 * (o + 1), :].rearrange("(p j) n -> p j n", j=PACK))
+
+        nc.vector.memset(scales[:].bitcast(I32), 0)
+        nc.sync.dma_start(var_sb[:], var)
+        nc.sync.dma_start(track_sb[:], track)
+        load_words(0)
+        nc.sync.dma_start(offs_sb[:], offs)
+        load_scales()
+        load_words(1)
+        load_weight(w2_raw, w2, 0)
+        load_weight(w2_raw, w2, 1)
+        nc.sync.dma_start(mean_sb[:], mean)
+        load_weight(w1_raw, w1, 0)
+        load_weight(w1_raw, w1, 1)
+
+        halves = [slice(h * HALF, (h + 1) * HALF) for h in range(2)]
+        list_halves = [slice(h * HALF // LIST_ROWS, (h + 1) * HALF // LIST_ROWS) for h in range(2)]
+
+        va = pool.tile([P, S], F32, name="va")
+        ln_va = pool.tile([P, S], F32, name="ln_va")
+        x_sc = pool.tile([P, S], U8, name="x_sc", align_bytes=64)
+        x0 = pool.tile([P, S], U32, name="x0", align_bytes=64)
+        x1 = [pool.tile([P, HALF], U32, name=f"x1_{h}", align_bytes=64) for h in range(2)]
+        warm = pool.tile([P, 1], F32, name="warm")
+
+        def tiles(name):
+            return [pool.tile([P, HALF], F32, name=f"{name}{h}") for h in range(2)]
+
+        logit, gain, shrink, y_sb, resid, corr, widen, result = [
+            tiles(n) for n in ("logit", "gain", "shrink", "y_sb", "resid", "corr", "widen", "result")
+        ]
+        gain[0] = pool.tile([P, HALF], F32, name="gain_first", tag="w1_raw1")
+        z_ps = [psum.tile([P, HALF], F32, name=f"z_ps{h}") for h in range(2)]
+        y_ps = [psum.tile([P, HALF], F32, name=f"y_ps{h}") for h in range(2)]
+
+        def cast(raw, o, name):
+            grouped = pool.tile([P, N * PACK], BF16, name=name, align_bytes=64)
+            nc.scalar.copy(
+                grouped[:].rearrange("p (c i j) -> p c j i", i=4, j=PACK),
+                raw[o][:].rearrange("p j (c i) -> p c j i", i=4),
+            )
+            return grouped
+
+        def quantize(grouped, name):
+            codes = pool.tile([P, N], U32, name=name + "_codes", align_bytes=64)
+            plane = pool.tile([P, N], U8, name=name + "_plane", align_bytes=64)
+            nc.vector.quantize_mx(out=codes[:].bitcast(FP8X4), scales=plane[:], in_=grouped[:])
+            return codes, plane
+
+        def product(acc, weight, o, h):
+            codes, plane = weight
+            moving = x0[:, halves[h]] if o == 0 else x1[h][:]
+            nc.tensor.matmul_mx(
+                out=acc[h][:],
+                lhsT=codes[:].bitcast(FP8X4),
+                lhsT_scale=plane[:],
+                rhs=moving.bitcast(FP8X4),
+                rhs_scale=x_sc[4 * o : P, halves[h]],
+                start=(o == 0),
+                stop=(o == PASSES - 1),
+            )
+
+        nc.vector.tensor_copy(va[:], var_sb[:].indirect(track_sb[:]))
+        nc.scalar.activation(ln_va[:], va[:], ACT.Ln)
+        nc.scalar.activation(warm[:], ln_va[:, 0:1], ACT.Sigmoid)
+        nc.vector.tensor_copy(x_sc[:], scales[:].indirect(offs_sb[:]))
+        nc.vector.tensor_copy(x0[:], words[0][:].bitcast(U32).indirect(offs_sb[:]))
+        q2 = [quantize(cast(w2_raw, o, f"w2g{o}"), f"w2q{o}") for o in range(PASSES)]
+        for h in range(2):
+            product(z_ps, q2[0], 0, h)
+        for h in range(2):
+            nc.vector.tensor_copy(x1[h][:], words[1][:].bitcast(U32).indirect(offs_sb[:, list_halves[h]]))
+            product(z_ps, q2[1], 1, h)
+        g1 = [cast(w1_raw, o, f"w1g{o}") for o in range(PASSES)]
+        for h in range(2):
+            nc.vector.tensor_tensor(logit[h][:], ln_va[:, halves[h]], z_ps[h][:], ALU.subtract)
+            nc.scalar.activation(gain[h][:], logit[h][:], ACT.Sigmoid)
+        q1 = [quantize(g1[o], f"w1q{o}") for o in range(PASSES)]
+        for o in range(PASSES):
+            for h in range(2):
+                product(y_ps, q1[o], o, h)
+        for h in range(2):
+            nc.vector.scalar_tensor_tensor(
+                shrink[h][:], gain[h][:], 1.0, va[:, halves[h]], ALU.subtract, ALU.mult
+            )
+        mu = y_sb
+        for h in range(2):
+            nc.vector.tensor_copy(mu[h][:], mean_sb[:].indirect(track_sb[:, list_halves[h]]))
+        for h in range(2):
+            nc.vector.tensor_tensor(resid[h][:], y_ps[h][:], mu[h][:], ALU.subtract)
+        for h in range(2):
+            nc.vector.tensor_tensor(corr[h][:], resid[h][:], gain[h][:], ALU.mult)
+            nc.scalar.activation(widen[h][:], corr[h][:], ACT.Square, scale=math.sqrt(0.1))
+        for h in range(2):
+            nc.vector.tensor_tensor(result[h][:], widen[h][:], shrink[h][:], ALU.subtract)
+            nc.sync.dma_start(out[:, halves[h]], result[h][:])

@@ -38,7 +38,7 @@ def tile_picked_ykal_var_p_kernel(
         words = [pool.tile([P, T], I32, name=f"words{o}") for o in range(PASSES)]
         scales = pool.tile([P, T], U8, name="scales")
         w1_raw = [pool.tile([P, PACK, N], F32, name=f"w1_raw{o}") for o in range(PASSES)]
-        w2_raw = [pool.tile([P, PACK, N], F32, name=f"w2_raw{o}") for o in range(PASSES)]
+        w2_all = pool.tile([P, PASSES, PACK, N], F32, name="w2_all")
 
         def load_words(o):
             nc.sync.dma_start(words[o][:], x_words[o].rearrange("p t b -> p (t b)").bitcast(I32))
@@ -50,8 +50,8 @@ def tile_picked_ykal_var_p_kernel(
                     x_scales[:, 4 * q : 4 * q + 4, :].bitcast(I32),
                 )
 
-        def load_weight(raw, w, o):
-            nc.sync.dma_start(raw[o][:], w[512 * o : 512 * (o + 1), :].rearrange("(p j) n -> p j n", j=PACK))
+        def load_weight(o):
+            nc.sync.dma_start(w1_raw[o][:], w1[512 * o : 512 * (o + 1), :].rearrange("(p j) n -> p j n", j=PACK))
 
         nc.vector.memset(scales[:].bitcast(I32), 0)
         nc.sync.dma_start(var_sb[:], var)
@@ -59,50 +59,46 @@ def tile_picked_ykal_var_p_kernel(
         load_words(0)
         nc.sync.dma_start(offs_sb[:], offs)
         load_scales()
+        nc.sync.dma_start(w2_all[:], w2.rearrange("(o p j) n -> p o j n", o=PASSES, j=PACK))
         load_words(1)
-        load_weight(w2_raw, w2, 0)
-        load_weight(w2_raw, w2, 1)
+        load_weight(0)
+        load_weight(1)
         nc.sync.dma_start(mean_sb[:], mean)
-        load_weight(w1_raw, w1, 0)
-        load_weight(w1_raw, w1, 1)
 
         halves = [slice(h * HALF, (h + 1) * HALF) for h in range(2)]
         list_halves = [slice(h * HALF // LIST_ROWS, (h + 1) * HALF // LIST_ROWS) for h in range(2)]
 
-        va = pool.tile([P, S], F32, name="va")
-        ln_va = pool.tile([P, S], F32, name="ln_va")
-        x_sc = pool.tile([P, S], U8, name="x_sc", align_bytes=64)
-        x0 = pool.tile([P, S], U32, name="x0", align_bytes=64)
-        x1 = [pool.tile([P, HALF], U32, name=f"x1_{h}", align_bytes=64) for h in range(2)]
-        warm = pool.tile([P, 1], F32, name="warm")
+        def tl(name, width=HALF, dtype=F32, **kw):
+            return pool.tile([P, width], dtype, name=name, **kw)
 
-        def tiles(name):
-            return [pool.tile([P, HALF], F32, name=f"{name}{h}") for h in range(2)]
-
-        logit, gain, shrink, y_sb, resid, corr, widen, result = [
-            tiles(n) for n in ("logit", "gain", "shrink", "y_sb", "resid", "corr", "widen", "result")
-        ]
-        gain[0] = pool.tile([P, HALF], F32, name="gain_first", tag="w1_raw1")
+        va = tl("va", S)
+        ln_va = tl("ln_va", S)
+        x_sc = tl("x_sc", S, U8, align_bytes=64)
+        x0 = tl("x0", S, U32, align_bytes=64)
+        x1 = tl("x1", S, U32, align_bytes=64)
+        warm = tl("warm", 1)
         z_ps = [psum.tile([P, HALF], F32, name=f"z_ps{h}") for h in range(2)]
-        y_ps = [psum.tile([P, HALF], F32, name=f"y_ps{h}") for h in range(2)]
+        y_ps = psum.tile([P, S], F32, name="y_ps")
 
-        def cast(raw, o, name):
-            grouped = pool.tile([P, N * PACK], BF16, name=name, align_bytes=64)
-            nc.scalar.copy(
-                grouped[:].rearrange("p (c i j) -> p c j i", i=4, j=PACK),
-                raw[o][:].rearrange("p j (c i) -> p c j i", i=4),
-            )
+        def cast(raw, name, eng):
+            grouped = tl(name, N * PACK, BF16, align_bytes=64)
+            dst = grouped[:].rearrange("p (c i j) -> p c j i", i=4, j=PACK)
+            src = raw.rearrange("p j (c i) -> p c j i", i=4)
+            if eng == "s":
+                nc.scalar.copy(dst, src)
+            else:
+                nc.vector.tensor_copy(dst, src)
             return grouped
 
         def quantize(grouped, name):
-            codes = pool.tile([P, N], U32, name=name + "_codes", align_bytes=64)
-            plane = pool.tile([P, N], U8, name=name + "_plane", align_bytes=64)
+            codes = tl(name + "_codes", N, U32, align_bytes=64)
+            plane = tl(name + "_plane", N, U8, align_bytes=64)
             nc.vector.quantize_mx(out=codes[:].bitcast(FP8X4), scales=plane[:], in_=grouped[:])
             return codes, plane
 
         def product(acc, weight, o, h):
             codes, plane = weight
-            moving = x0[:, halves[h]] if o == 0 else x1[h][:]
+            moving = x0[:, halves[h]] if o == 0 else x1[:, halves[h]]
             nc.tensor.matmul_mx(
                 out=acc[h][:],
                 lhsT=codes[:].bitcast(FP8X4),
@@ -118,32 +114,48 @@ def tile_picked_ykal_var_p_kernel(
         nc.scalar.activation(warm[:], ln_va[:, 0:1], ACT.Sigmoid)
         nc.vector.tensor_copy(x_sc[:], scales[:].indirect(offs_sb[:]))
         nc.vector.tensor_copy(x0[:], words[0][:].bitcast(U32).indirect(offs_sb[:]))
-        q2 = [quantize(cast(w2_raw, o, f"w2g{o}"), f"w2q{o}") for o in range(PASSES)]
+        q2 = [quantize(cast(w2_all[:, o, :, :], f"w2g{o}", "s"), f"w2q{o}") for o in range(PASSES)]
         for h in range(2):
             product(z_ps, q2[0], 0, h)
         for h in range(2):
-            nc.vector.tensor_copy(x1[h][:], words[1][:].bitcast(U32).indirect(offs_sb[:, list_halves[h]]))
+            nc.vector.tensor_copy(x1[:, halves[h]], words[1][:].bitcast(U32).indirect(offs_sb[:, list_halves[h]]))
             product(z_ps, q2[1], 1, h)
-        g1 = [cast(w1_raw, o, f"w1g{o}") for o in range(PASSES)]
-        for h in range(2):
-            nc.vector.tensor_tensor(logit[h][:], ln_va[:, halves[h]], z_ps[h][:], ALU.subtract)
-            nc.scalar.activation(gain[h][:], logit[h][:], ACT.Sigmoid)
+        g1 = [cast(w1_raw[o][:], f"w1g{o}", "s") for o in range(PASSES)]
         q1 = [quantize(g1[o], f"w1q{o}") for o in range(PASSES)]
+        late = pool.tile([P, 4, HALF], F32, name="late", tag="w1_raw1")
+        logit = [tl("logit0", tag="w1_raw0")[:], late[:, 1, :]]
+        gain = [late[:, 0, :], tl("gain1")[:]]
+        for h in range(2):
+            nc.vector.tensor_tensor(logit[h], ln_va[:, halves[h]], z_ps[h][:], ALU.subtract)
+            nc.scalar.activation(gain[h], logit[h], ACT.Sigmoid)
+
         for o in range(PASSES):
-            for h in range(2):
-                product(y_ps, q1[o], o, h)
+            nc.tensor.matmul_mx(
+                out=y_ps[:],
+                lhsT=q1[o][0][:].bitcast(FP8X4),
+                lhsT_scale=q1[o][1][:],
+                rhs=(x0, x1)[o][:].bitcast(FP8X4),
+                rhs_scale=x_sc[4 * o : P, :],
+                start=(o == 0),
+                stop=(o == PASSES - 1),
+            )
+        mu = [late[:, 2, :], late[:, 3, :]]
+        for h in range(2):
+            nc.vector.tensor_copy(mu[h], mean_sb[:].indirect(track_sb[:, list_halves[h]]))
+        resid = [tl(f"resid{h}") for h in range(2)]
+        corr = [tl(f"corr{h}") for h in range(2)]
+        widen = [tl(f"widen{h}") for h in range(2)]
+        result = [tl(f"result{h}") for h in range(2)]
+        for h in range(2):
+            nc.vector.tensor_tensor(resid[h][:], y_ps[:, halves[h]], mu[h], ALU.subtract)
+        for h in range(2):
+            nc.vector.tensor_tensor(corr[h][:], resid[h][:], gain[h], ALU.mult)
+            nc.scalar.activation(widen[h][:], corr[h][:], ACT.Square, scale=math.sqrt(0.1))
+        shrink = pool.tile([P, 2, HALF], F32, name="shrink", tag="resid0")
         for h in range(2):
             nc.vector.scalar_tensor_tensor(
-                shrink[h][:], gain[h][:], 1.0, va[:, halves[h]], ALU.subtract, ALU.mult
+                shrink[:, h, :], gain[h], 1.0, va[:, halves[h]], ALU.subtract, ALU.mult
             )
-        mu = y_sb
         for h in range(2):
-            nc.vector.tensor_copy(mu[h][:], mean_sb[:].indirect(track_sb[:, list_halves[h]]))
-        for h in range(2):
-            nc.vector.tensor_tensor(resid[h][:], y_ps[h][:], mu[h][:], ALU.subtract)
-        for h in range(2):
-            nc.vector.tensor_tensor(corr[h][:], resid[h][:], gain[h][:], ALU.mult)
-            nc.scalar.activation(widen[h][:], corr[h][:], ACT.Square, scale=math.sqrt(0.1))
-        for h in range(2):
-            nc.vector.tensor_tensor(result[h][:], widen[h][:], shrink[h][:], ALU.subtract)
+            nc.vector.tensor_tensor(result[h][:], widen[h][:], shrink[:, h, :], ALU.subtract)
             nc.sync.dma_start(out[:, halves[h]], result[h][:])

@@ -43,22 +43,24 @@ def tile_picked_ykal_var_p_kernel(
         def load_words(o):
             nc.sync.dma_start(words[o][:], x_words[o].rearrange("p t b -> p (t b)").bitcast(I32))
 
-        def load_scales():
+        def load_scales(o):
             for q in range(4):
                 nc.sync.dma_start(
-                    scales[32 * q : 32 * q + 8, :].bitcast(I32),
-                    x_scales[:, 4 * q : 4 * q + 4, :].bitcast(I32),
+                    scales[32 * q + 4 * o : 32 * q + 4 * o + 4, :].bitcast(I32),
+                    x_scales[o, 4 * q : 4 * q + 4, :].bitcast(I32),
                 )
 
         def load_weight(o):
             nc.sync.dma_start(w1_raw[o][:], w1[512 * o : 512 * (o + 1), :].rearrange("(p j) n -> p j n", j=PACK))
 
-        nc.vector.memset(scales[:].bitcast(I32), 0)
+        nc.vector.memset(scales[:, : T // 2].bitcast(I32), 0)
+        nc.gpsimd.memset(scales[:, T // 2 :].bitcast(I32), 0)
         nc.sync.dma_start(var_sb[:], var)
         nc.sync.dma_start(track_sb[:], track)
-        load_words(0)
         nc.sync.dma_start(offs_sb[:], offs)
-        load_scales()
+        load_scales(0)
+        load_words(0)
+        load_scales(1)
         nc.sync.dma_start(w2_all[:], w2.rearrange("(o p j) n -> p o j n", o=PASSES, j=PACK))
         load_words(1)
         load_weight(0)
@@ -76,7 +78,6 @@ def tile_picked_ykal_var_p_kernel(
         x_sc = tl("x_sc", S, U8, align_bytes=64)
         x0 = tl("x0", S, U32, align_bytes=64)
         x1 = tl("x1", S, U32, align_bytes=64)
-        warm = tl("warm", 1)
         z_ps = [psum.tile([P, HALF], F32, name=f"z_ps{h}") for h in range(2)]
         y_ps = psum.tile([P, S], F32, name="y_ps")
 
@@ -111,7 +112,6 @@ def tile_picked_ykal_var_p_kernel(
 
         nc.vector.tensor_copy(va[:], var_sb[:].indirect(track_sb[:]))
         nc.scalar.activation(ln_va[:], va[:], ACT.Ln)
-        nc.scalar.activation(warm[:], ln_va[:, 0:1], ACT.Sigmoid)
         nc.vector.tensor_copy(x_sc[:], scales[:].indirect(offs_sb[:]))
         nc.vector.tensor_copy(x0[:], words[0][:].bitcast(U32).indirect(offs_sb[:]))
         q2 = [quantize(cast(w2_all[:, o, :, :], f"w2g{o}", "s"), f"w2q{o}") for o in range(PASSES)]

@@ -43,12 +43,13 @@ def tile_picked_ykal_var_p_kernel(
         def load_words(o):
             nc.sync.dma_start(words[o][:], x_words[o].rearrange("p t b -> p (t b)").bitcast(I32))
 
-        def load_scales(o):
-            for q in range(4):
-                nc.sync.dma_start(
-                    scales[32 * q + 4 * o : 32 * q + 4 * o + 4, :].bitcast(I32),
-                    x_scales[o, 4 * q : 4 * q + 4, :].bitcast(I32),
-                )
+        def load_scales(half):
+            for j in (2 * half, 2 * half + 1):
+                for o in range(PASSES):
+                    nc.sync.dma_start(
+                        scales[4 * o + j : P : 32, :].bitcast(I32),
+                        x_scales[o, j:16:4, :].bitcast(I32),
+                    )
 
         def load_weight(o):
             nc.sync.dma_start(w1_raw[o][:], w1[512 * o : 512 * (o + 1), :].rearrange("(p j) n -> p j n", j=PACK))

@@ -80,7 +80,7 @@ def tile_picked_ykal_var_p_kernel(
         x0 = tl("x0", S, U32, align_bytes=64)
         x1 = tl("x1", S, U32, align_bytes=64)
         z_ps = [psum.tile([P, HALF], F32, name=f"z_ps{h}") for h in range(2)]
-        y_ps = psum.tile([P, S], F32, name="y_ps")
+        y_ps = [psum.tile([P, HALF], F32, name=f"y_ps{h}") for h in range(2)]
 
         def cast(raw, name, eng):
             grouped = tl(name, N * PACK, BF16, align_bytes=64)
@@ -113,6 +113,8 @@ def tile_picked_ykal_var_p_kernel(
 
         nc.vector.tensor_copy(va[:], var_sb[:].indirect(track_sb[:]))
         nc.scalar.activation(ln_va[:], va[:], ACT.Ln)
+        warm = tl("warm", 1)
+        nc.scalar.activation(warm[:], ln_va[:, 0:1], ACT.Sigmoid)
         nc.vector.tensor_copy(x_sc[:], scales[:].indirect(offs_sb[:]))
         nc.vector.tensor_copy(x0[:], words[0][:].bitcast(U32).indirect(offs_sb[:]))
         q2 = [quantize(cast(w2_all[:, o, :, :], f"w2g{o}", "s"), f"w2q{o}") for o in range(PASSES)]
@@ -129,17 +131,9 @@ def tile_picked_ykal_var_p_kernel(
         for h in range(2):
             nc.vector.tensor_tensor(logit[h], ln_va[:, halves[h]], z_ps[h][:], ALU.subtract)
             nc.scalar.activation(gain[h], logit[h], ACT.Sigmoid)
-
         for o in range(PASSES):
-            nc.tensor.matmul_mx(
-                out=y_ps[:],
-                lhsT=q1[o][0][:].bitcast(FP8X4),
-                lhsT_scale=q1[o][1][:],
-                rhs=(x0, x1)[o][:].bitcast(FP8X4),
-                rhs_scale=x_sc[4 * o : P, :],
-                start=(o == 0),
-                stop=(o == PASSES - 1),
-            )
+            for h in range(2):
+                product(y_ps, q1[o], o, h)
         mu = [late[:, 2, :], late[:, 3, :]]
         for h in range(2):
             nc.vector.tensor_copy(mu[h], mean_sb[:].indirect(track_sb[:, list_halves[h]]))
@@ -148,7 +142,7 @@ def tile_picked_ykal_var_p_kernel(
         widen = [tl(f"widen{h}") for h in range(2)]
         result = [tl(f"result{h}") for h in range(2)]
         for h in range(2):
-            nc.vector.tensor_tensor(resid[h][:], y_ps[:, halves[h]], mu[h], ALU.subtract)
+            nc.vector.tensor_tensor(resid[h][:], y_ps[h][:], mu[h], ALU.subtract)
         for h in range(2):
             nc.vector.tensor_tensor(corr[h][:], resid[h][:], gain[h], ALU.mult)
             nc.scalar.activation(widen[h][:], corr[h][:], ACT.Square, scale=math.sqrt(0.1))

@@ -146,11 +146,13 @@ def tile_picked_ykal_var_p_kernel(
         for h in range(2):
             nc.vector.tensor_tensor(corr[h][:], resid[h][:], gain[h], ALU.mult)
             nc.scalar.activation(widen[h][:], corr[h][:], ACT.Square, scale=math.sqrt(0.1))
-        shrink = pool.tile([P, 2, HALF], F32, name="shrink", tag="resid0")
-        for h in range(2):
-            nc.vector.scalar_tensor_tensor(
-                shrink[:, h, :], gain[h], 1.0, va[:, halves[h]], ALU.subtract, ALU.mult
-            )
-        for h in range(2):
-            nc.vector.tensor_tensor(result[h][:], widen[h][:], shrink[:, h, :], ALU.subtract)
-            nc.sync.dma_start(out[:, halves[h]], result[h][:])
+        keep0 = tl("keep0")
+        nc.scalar.activation(keep0[:], logit[0], ACT.Sigmoid, scale=-1.0)
+        base0 = tl("base0")
+        nc.gpsimd.tensor_tensor(base0[:], keep0[:], va[:, halves[0]], ALU.mult)
+        shrink = tl("shrink", tag="resid0")
+        nc.vector.scalar_tensor_tensor(shrink[:], gain[1], 1.0, va[:, halves[1]], ALU.subtract, ALU.mult)
+        nc.vector.tensor_tensor(result[0][:], widen[0][:], base0[:], ALU.add)
+        nc.sync.dma_start(out[:, halves[0]], result[0][:])
+        nc.vector.tensor_tensor(result[1][:], widen[1][:], shrink[:], ALU.subtract)
+        nc.sync.dma_start(out[:, halves[1]], result[1][:])

@@ -18,9 +18,13 @@ ACT = mybir.ActivationFunctionType
 
 P = 128
 PACK = 4
-PASSES = 2
-HALF = S // 2
+K_PASS = P * PACK
+PASSES = K // K_PASS
+QUADRANT = 32
+PLANE_ROWS = 4
 LIST_ROWS = 16
+HALF = S // 2
+RUN = 4
 
 
 def tile_picked_ykal_var_p_kernel(
@@ -38,121 +42,126 @@ def tile_picked_ykal_var_p_kernel(
         words = [pool.tile([P, T], I32, name=f"words{o}") for o in range(PASSES)]
         scales = pool.tile([P, T], U8, name="scales")
         w1_raw = [pool.tile([P, PACK, N], F32, name=f"w1_raw{o}") for o in range(PASSES)]
-        w2_all = pool.tile([P, PASSES, PACK, N], F32, name="w2_all")
+        w2_raw = pool.tile([P, PASSES, PACK, N], F32, name="w2_raw")
 
         def load_words(o):
             nc.sync.dma_start(words[o][:], x_words[o].rearrange("p t b -> p (t b)").bitcast(I32))
 
-        def load_scales(half):
-            for j in (2 * half, 2 * half + 1):
+        def load_scales(rows):
+            for j in rows:
                 for o in range(PASSES):
                     nc.sync.dma_start(
-                        scales[4 * o + j : P : 32, :].bitcast(I32),
-                        x_scales[o, j:16:4, :].bitcast(I32),
+                        scales[PLANE_ROWS * o + j : P : QUADRANT, :].bitcast(I32),
+                        x_scales[o, j : K_PASS // 32 : PLANE_ROWS, :].bitcast(I32),
                     )
 
-        def load_weight(o):
-            nc.sync.dma_start(w1_raw[o][:], w1[512 * o : 512 * (o + 1), :].rearrange("(p j) n -> p j n", j=PACK))
+        def load_w1(o):
+            rows = w1[K_PASS * o : K_PASS * (o + 1), :]
+            nc.sync.dma_start(w1_raw[o][:], rows.rearrange("(p j) n -> p j n", j=PACK))
 
         nc.vector.memset(scales[:, : T // 2].bitcast(I32), 0)
         nc.gpsimd.memset(scales[:, T // 2 :].bitcast(I32), 0)
+
         nc.sync.dma_start(var_sb[:], var)
         nc.sync.dma_start(track_sb[:], track)
         nc.sync.dma_start(offs_sb[:], offs)
-        load_scales(0)
+        load_scales(range(0, PLANE_ROWS // 2))
         load_words(0)
-        load_scales(1)
-        nc.sync.dma_start(w2_all[:], w2.rearrange("(o p j) n -> p o j n", o=PASSES, j=PACK))
+        load_scales(range(PLANE_ROWS // 2, PLANE_ROWS))
+        nc.sync.dma_start(w2_raw[:], w2.rearrange("(o p j) n -> p o j n", o=PASSES, j=PACK))
         load_words(1)
-        load_weight(0)
-        load_weight(1)
+        load_w1(0)
+        load_w1(1)
         nc.sync.dma_start(mean_sb[:], mean)
 
         halves = [slice(h * HALF, (h + 1) * HALF) for h in range(2)]
         list_halves = [slice(h * HALF // LIST_ROWS, (h + 1) * HALF // LIST_ROWS) for h in range(2)]
 
-        def tl(name, width=HALF, dtype=F32, **kw):
-            return pool.tile([P, width], dtype, name=name, **kw)
+        def new_tile(name, width=HALF, dtype=F32, **options):
+            return pool.tile([P, width], dtype, name=name, **options)
 
-        va = tl("va", S)
-        ln_va = tl("ln_va", S)
-        x_sc = tl("x_sc", S, U8, align_bytes=64)
-        x0 = tl("x0", S, U32, align_bytes=64)
-        x1 = tl("x1", S, U32, align_bytes=64)
+        va = new_tile("va", S)
+        ln_va = new_tile("ln_va", S)
+        picked_scales = new_tile("picked_scales", S, U8, align_bytes=64)
+        picked_words = [new_tile(f"picked_words{o}", S, U32, align_bytes=64) for o in range(PASSES)]
         z_ps = [psum.tile([P, HALF], F32, name=f"z_ps{h}") for h in range(2)]
         y_ps = [psum.tile([P, HALF], F32, name=f"y_ps{h}") for h in range(2)]
 
-        def cast(raw, name, eng):
-            grouped = tl(name, N * PACK, BF16, align_bytes=64)
-            dst = grouped[:].rearrange("p (c i j) -> p c j i", i=4, j=PACK)
-            src = raw.rearrange("p j (c i) -> p c j i", i=4)
-            if eng == "s":
-                nc.scalar.copy(dst, src)
-            else:
-                nc.vector.tensor_copy(dst, src)
+        def round_weights(raw, name):
+            grouped = new_tile(name, N * PACK, BF16, align_bytes=64)
+            nc.scalar.copy(
+                grouped[:].rearrange("p (c i j) -> p c j i", i=RUN, j=PACK),
+                raw.rearrange("p j (c i) -> p c j i", i=RUN),
+            )
             return grouped
 
         def quantize(grouped, name):
-            codes = tl(name + "_codes", N, U32, align_bytes=64)
-            plane = tl(name + "_plane", N, U8, align_bytes=64)
+            codes = new_tile(name + "_codes", N, U32, align_bytes=64)
+            plane = new_tile(name + "_plane", N, U8, align_bytes=64)
             nc.vector.quantize_mx(out=codes[:].bitcast(FP8X4), scales=plane[:], in_=grouped[:])
             return codes, plane
 
         def product(acc, weight, o, h):
             codes, plane = weight
-            moving = x0[:, halves[h]] if o == 0 else x1[:, halves[h]]
             nc.tensor.matmul_mx(
                 out=acc[h][:],
                 lhsT=codes[:].bitcast(FP8X4),
                 lhsT_scale=plane[:],
-                rhs=moving.bitcast(FP8X4),
-                rhs_scale=x_sc[4 * o : P, halves[h]],
+                rhs=picked_words[o][:, halves[h]].bitcast(FP8X4),
+                rhs_scale=picked_scales[PLANE_ROWS * o : P, halves[h]],
                 start=(o == 0),
                 stop=(o == PASSES - 1),
             )
 
         nc.vector.tensor_copy(va[:], var_sb[:].indirect(track_sb[:]))
         nc.scalar.activation(ln_va[:], va[:], ACT.Ln)
-        warm = tl("warm", 1)
-        nc.scalar.activation(warm[:], ln_va[:, 0:1], ACT.Sigmoid)
-        nc.vector.tensor_copy(x_sc[:], scales[:].indirect(offs_sb[:]))
-        nc.vector.tensor_copy(x0[:], words[0][:].bitcast(U32).indirect(offs_sb[:]))
-        q2 = [quantize(cast(w2_all[:, o, :, :], f"w2g{o}", "s"), f"w2q{o}") for o in range(PASSES)]
+        warm_up = new_tile("warm_up", 1)
+        nc.scalar.activation(warm_up[:], ln_va[:, 0:1], ACT.Sigmoid)
+
+        nc.vector.tensor_copy(picked_scales[:], scales[:].indirect(offs_sb[:]))
+        nc.vector.tensor_copy(picked_words[0][:], words[0][:].bitcast(U32).indirect(offs_sb[:]))
+        w2_mx = [quantize(round_weights(w2_raw[:, o, :, :], f"w2_bf{o}"), f"w2_mx{o}") for o in range(PASSES)]
         for h in range(2):
-            product(z_ps, q2[0], 0, h)
+            product(z_ps, w2_mx[0], 0, h)
         for h in range(2):
-            nc.vector.tensor_copy(x1[:, halves[h]], words[1][:].bitcast(U32).indirect(offs_sb[:, list_halves[h]]))
-            product(z_ps, q2[1], 1, h)
-        g1 = [cast(w1_raw[o][:], f"w1g{o}", "s") for o in range(PASSES)]
-        q1 = [quantize(g1[o], f"w1q{o}") for o in range(PASSES)]
-        late = pool.tile([P, 4, HALF], F32, name="late", tag="w1_raw1")
-        logit = [tl("logit0", tag="w1_raw0")[:], late[:, 1, :]]
-        gain = [late[:, 0, :], tl("gain1")[:]]
+            nc.vector.tensor_copy(
+                picked_words[1][:, halves[h]], words[1][:].bitcast(U32).indirect(offs_sb[:, list_halves[h]])
+            )
+            product(z_ps, w2_mx[1], 1, h)
+        w1_bf = [round_weights(w1_raw[o][:], f"w1_bf{o}") for o in range(PASSES)]
+        w1_mx = [quantize(w1_bf[o], f"w1_mx{o}") for o in range(PASSES)]
+
+        after_w1 = pool.tile([P, 5, HALF], F32, name="after_w1", tag="w1_raw1")
+        logit = [new_tile("logit0", tag="w1_raw0")[:], after_w1[:, 1, :]]
+        gain = [after_w1[:, 0, :], new_tile("gain1")[:]]
+        mu = [after_w1[:, 2, :], after_w1[:, 3, :]]
+        z1_sb = after_w1[:, 4, :]
+
+        nc.vector.tensor_tensor(logit[0], ln_va[:, halves[0]], z_ps[0][:], ALU.subtract)
+        nc.scalar.copy(z1_sb, z_ps[1][:])
+        nc.gpsimd.tensor_tensor(logit[1], ln_va[:, halves[1]], z1_sb, ALU.subtract)
         for h in range(2):
-            nc.vector.tensor_tensor(logit[h], ln_va[:, halves[h]], z_ps[h][:], ALU.subtract)
             nc.scalar.activation(gain[h], logit[h], ACT.Sigmoid)
         for o in range(PASSES):
             for h in range(2):
-                product(y_ps, q1[o], o, h)
-        mu = [late[:, 2, :], late[:, 3, :]]
+                product(y_ps, w1_mx[o], o, h)
+
         for h in range(2):
             nc.vector.tensor_copy(mu[h], mean_sb[:].indirect(track_sb[:, list_halves[h]]))
-        resid = [tl(f"resid{h}") for h in range(2)]
-        corr = [tl(f"corr{h}") for h in range(2)]
-        widen = [tl(f"widen{h}") for h in range(2)]
-        result = [tl(f"result{h}") for h in range(2)]
+        resid = [new_tile(f"resid{h}") for h in range(2)]
+        corr = [new_tile(f"corr{h}") for h in range(2)]
+        widen = [new_tile(f"widen{h}") for h in range(2)]
+        result = [new_tile(f"result{h}") for h in range(2)]
         for h in range(2):
             nc.vector.tensor_tensor(resid[h][:], y_ps[h][:], mu[h], ALU.subtract)
         for h in range(2):
             nc.vector.tensor_tensor(corr[h][:], resid[h][:], gain[h], ALU.mult)
             nc.scalar.activation(widen[h][:], corr[h][:], ACT.Square, scale=math.sqrt(0.1))
-        keep0 = tl("keep0")
-        nc.scalar.activation(keep0[:], logit[0], ACT.Sigmoid, scale=-1.0)
-        base0 = tl("base0")
-        nc.gpsimd.tensor_tensor(base0[:], keep0[:], va[:, halves[0]], ALU.mult)
-        shrink = tl("shrink", tag="resid0")
-        nc.vector.scalar_tensor_tensor(shrink[:], gain[1], 1.0, va[:, halves[1]], ALU.subtract, ALU.mult)
-        nc.vector.tensor_tensor(result[0][:], widen[0][:], base0[:], ALU.add)
-        nc.sync.dma_start(out[:, halves[0]], result[0][:])
-        nc.vector.tensor_tensor(result[1][:], widen[1][:], shrink[:], ALU.subtract)
-        nc.sync.dma_start(out[:, halves[1]], result[1][:])
+        shrink = pool.tile([P, 2, HALF], F32, name="shrink", tag="resid0")
+        for h in range(2):
+            nc.vector.scalar_tensor_tensor(
+                shrink[:, h, :], gain[h], 1.0, va[:, halves[h]], ALU.subtract, ALU.mult
+            )
+        for h in range(2):
+            nc.vector.tensor_tensor(result[h][:], widen[h][:], shrink[:, h, :], ALU.subtract)
+            nc.sync.dma_start(out[:, halves[h]], result[h][:])

@@ -33,46 +33,38 @@ def tile_picked_ykal_var_p_kernel(
     nc = tc.nc
     with ExitStack() as ctx:
         pool = ctx.enter_context(tc.tile_pool(name="keep", bufs=1))
+        late = ctx.enter_context(tc.tile_pool(name="late", bufs=1))
         psum = ctx.enter_context(tc.psum_pool(name="psum", bufs=1))
 
         offs_sb = pool.tile([P, S // LIST_ROWS], U16, name="offs_sb")
         track_sb = pool.tile([P, S // LIST_ROWS], U16, name="track_sb")
         var_sb = pool.tile([P, U], F32, name="var_sb")
-        mean_sb = pool.tile([P, U], F32, name="mean_sb")
         words = [pool.tile([P, T], I32, name=f"words{o}") for o in range(PASSES)]
-        scales = pool.tile([P, T], U8, name="scales")
-        w1_raw = [pool.tile([P, PACK, N], F32, name=f"w1_raw{o}") for o in range(PASSES)]
+        scales = late.tile([P, PASSES, T], U8, name="scales", offset=2048)
+        w1_raw = [late.tile([P, PACK, N], F32, name="w1_raw0", offset=0)]
+        planes = pool.tile([P, PASSES, S], U8, name="planes", align_bytes=64)
         w2_raw = pool.tile([P, PASSES, PACK, N], F32, name="w2_raw")
 
         def load_words(o):
             nc.sync.dma_start(words[o][:], x_words[o].rearrange("p t b -> p (t b)").bitcast(I32))
 
-        def load_scales(rows):
-            for j in rows:
-                for o in range(PASSES):
-                    nc.sync.dma_start(
-                        scales[PLANE_ROWS * o + j : P : QUADRANT, :].bitcast(I32),
-                        x_scales[o, j : K_PASS // 32 : PLANE_ROWS, :].bitcast(I32),
-                    )
-
         def load_w1(o):
             rows = w1[K_PASS * o : K_PASS * (o + 1), :]
             nc.sync.dma_start(w1_raw[o][:], rows.rearrange("(p j) n -> p j n", j=PACK))
 
-        nc.vector.memset(scales[:, : T // 2].bitcast(I32), 0)
-        nc.gpsimd.memset(scales[:, T // 2 :].bitcast(I32), 0)
+        flat = scales[:].rearrange("p o t -> p (o t)").bitcast(I32)
+        nc.vector.memset(flat[:, :640], 0)
+        nc.gpsimd.memset(flat[:, 640:], 0)
+        nc.gpsimd.memset(planes[:].rearrange("p o s -> p (o s)").bitcast(I32), 0)
 
         nc.sync.dma_start(var_sb[:], var)
         nc.sync.dma_start(track_sb[:], track)
         nc.sync.dma_start(offs_sb[:], offs)
-        load_scales(range(0, PLANE_ROWS // 2))
+        nc.sync.dma_start(scales[4:P:8, :, :].bitcast(I32), x_scales.rearrange("o r t -> r o t").bitcast(I32))
         load_words(0)
-        load_scales(range(PLANE_ROWS // 2, PLANE_ROWS))
         nc.sync.dma_start(w2_raw[:], w2.rearrange("(o p j) n -> p o j n", o=PASSES, j=PACK))
         load_words(1)
         load_w1(0)
-        load_w1(1)
-        nc.sync.dma_start(mean_sb[:], mean)
 
         halves = [slice(h * HALF, (h + 1) * HALF) for h in range(2)]
         list_halves = [slice(h * HALF // LIST_ROWS, (h + 1) * HALF // LIST_ROWS) for h in range(2)]
@@ -82,7 +74,7 @@ def tile_picked_ykal_var_p_kernel(
 
         va = new_tile("va", S)
         ln_va = new_tile("ln_va", S)
-        picked_scales = new_tile("picked_scales", S, U8, align_bytes=64)
+        picked_scales = pool.tile([P, PASSES, S], U8, name="picked_scales", align_bytes=64)
         picked_words = [new_tile(f"picked_words{o}", S, U32, align_bytes=64) for o in range(PASSES)]
         z_ps = [psum.tile([P, HALF], F32, name=f"z_ps{h}") for h in range(2)]
         y_ps = [psum.tile([P, HALF], F32, name=f"y_ps{h}") for h in range(2)]
@@ -108,7 +100,7 @@ def tile_picked_ykal_var_p_kernel(
                 lhsT=codes[:].bitcast(FP8X4),
                 lhsT_scale=plane[:],
                 rhs=picked_words[o][:, halves[h]].bitcast(FP8X4),
-                rhs_scale=picked_scales[PLANE_ROWS * o : P, halves[h]],
+                rhs_scale=planes[:, o, halves[h]],
                 start=(o == 0),
                 stop=(o == PASSES - 1),
             )
@@ -118,24 +110,35 @@ def tile_picked_ykal_var_p_kernel(
         warm_up = new_tile("warm_up", 1)
         nc.scalar.activation(warm_up[:], ln_va[:, 0:1], ACT.Sigmoid)
 
-        nc.vector.tensor_copy(picked_scales[:], scales[:].indirect(offs_sb[:]))
+        for o in range(PASSES):
+            nc.vector.tensor_copy(picked_scales[:, o, :], scales[:, o, :].indirect(offs_sb[:]))
+        for j in range(PLANE_ROWS):
+            nc.sync.dma_start(
+                planes[j:P:QUADRANT].rearrange("p o s -> p (o s)").bitcast(I32),
+                picked_scales[4 + 8 * j : P : QUADRANT].rearrange("p o s -> p (o s)").bitcast(I32),
+            )
+        w1_raw.append(late.tile([P, PACK, N], F32, name="w1_raw1", offset=2048))
+        mean_sb = late.tile([P, U], F32, name="mean_sb", offset=4096)
+        load_w1(1)
+        nc.sync.dma_start(mean_sb[:], mean)
         nc.vector.tensor_copy(picked_words[0][:], words[0][:].bitcast(U32).indirect(offs_sb[:]))
         w2_mx = [quantize(round_weights(w2_raw[:, o, :, :], f"w2_bf{o}"), f"w2_mx{o}") for o in range(PASSES)]
-        for h in range(2):
-            product(z_ps, w2_mx[0], 0, h)
         for h in range(2):
             nc.vector.tensor_copy(
                 picked_words[1][:, halves[h]], words[1][:].bitcast(U32).indirect(offs_sb[:, list_halves[h]])
             )
-            product(z_ps, w2_mx[1], 1, h)
+            for o in range(PASSES):
+                product(z_ps, w2_mx[o], o, h)
         w1_bf = [round_weights(w1_raw[o][:], f"w1_bf{o}") for o in range(PASSES)]
         w1_mx = [quantize(w1_bf[o], f"w1_mx{o}") for o in range(PASSES)]
 
-        after_w1 = pool.tile([P, 5, HALF], F32, name="after_w1", tag="w1_raw1")
-        logit = [new_tile("logit0", tag="w1_raw0")[:], after_w1[:, 1, :]]
-        gain = [after_w1[:, 0, :], new_tile("gain1")[:]]
-        mu = [after_w1[:, 2, :], after_w1[:, 3, :]]
-        z1_sb = after_w1[:, 4, :]
+        gain0 = late.tile([P, HALF], F32, name="gain0", offset=2048)
+        z1 = late.tile([P, HALF], F32, name="z1", offset=3072)
+        logit0 = late.tile([P, HALF], F32, name="logit0", offset=0)
+        logit = [logit0[:], new_tile("logit1")[:]]
+        gain = [gain0[:], new_tile("gain1")[:]]
+        mu = [new_tile("mu0")[:], new_tile("mu1")[:]]
+        z1_sb = z1[:]
 
         nc.vector.tensor_tensor(logit[0], ln_va[:, halves[0]], z_ps[0][:], ALU.subtract)
         nc.scalar.copy(z1_sb, z_ps[1][:])

@@ -61,8 +61,8 @@ def tile_picked_ykal_var_p_kernel(
         nc.sync.dma_start(track_sb[:], track)
         nc.sync.dma_start(offs_sb[:], offs)
         nc.sync.dma_start(scales[4:P:8, :, :].bitcast(I32), x_scales.rearrange("o r t -> r o t").bitcast(I32))
-        load_words(0)
         nc.sync.dma_start(w2_raw[:], w2.rearrange("(o p j) n -> p o j n", o=PASSES, j=PACK))
+        load_words(0)
         load_words(1)
         load_w1(0)
 
@@ -72,7 +72,6 @@ def tile_picked_ykal_var_p_kernel(
         def new_tile(name, width=HALF, dtype=F32, **options):
             return pool.tile([P, width], dtype, name=name, **options)
 
-        va = new_tile("va", S)
         ln_va = new_tile("ln_va", S)
         picked_scales = pool.tile([P, PASSES, S], U8, name="picked_scales", align_bytes=64)
         picked_words = [new_tile(f"picked_words{o}", S, U32, align_bytes=64) for o in range(PASSES)]
@@ -105,10 +104,8 @@ def tile_picked_ykal_var_p_kernel(
                 stop=(o == PASSES - 1),
             )
 
-        nc.vector.tensor_copy(va[:], var_sb[:].indirect(track_sb[:]))
-        nc.scalar.activation(ln_va[:], va[:], ACT.Ln)
-        warm_up = new_tile("warm_up", 1)
-        nc.scalar.activation(warm_up[:], ln_va[:, 0:1], ACT.Sigmoid)
+        ln_var = new_tile("ln_var", U)
+        nc.scalar.activation(ln_var[:], var_sb[:], ACT.Ln)
 
         for o in range(PASSES):
             nc.vector.tensor_copy(picked_scales[:, o, :], scales[:, o, :].indirect(offs_sb[:]))
@@ -121,8 +118,11 @@ def tile_picked_ykal_var_p_kernel(
         mean_sb = late.tile([P, U], F32, name="mean_sb", offset=4096)
         load_w1(1)
         nc.sync.dma_start(mean_sb[:], mean)
-        nc.vector.tensor_copy(picked_words[0][:], words[0][:].bitcast(U32).indirect(offs_sb[:]))
+        nc.vector.tensor_copy(ln_va[:], ln_var[:].indirect(track_sb[:]))
         w2_mx = [quantize(round_weights(w2_raw[:, o, :, :], f"w2_bf{o}"), f"w2_mx{o}") for o in range(PASSES)]
+        va = new_tile("va", S, tag="w2_raw")
+        nc.scalar.activation(va[:], ln_va[:], ACT.Exp, bias=-math.log(2.0))
+        nc.vector.tensor_copy(picked_words[0][:], words[0][:].bitcast(U32).indirect(offs_sb[:]))
         for h in range(2):
             nc.vector.tensor_copy(
                 picked_words[1][:, halves[h]], words[1][:].bitcast(U32).indirect(offs_sb[:, list_halves[h]])
@@ -144,7 +144,7 @@ def tile_picked_ykal_var_p_kernel(
         nc.scalar.copy(z1_sb, z_ps[1][:])
         nc.gpsimd.tensor_tensor(logit[1], ln_va[:, halves[1]], z1_sb, ALU.subtract)
         for h in range(2):
-            nc.scalar.activation(gain[h], logit[h], ACT.Sigmoid)
+            nc.scalar.activation(gain[h], logit[h], ACT.Tanh, scale=0.5)
         for o in range(PASSES):
             for h in range(2):
                 product(y_ps, w1_mx[o], o, h)
@@ -158,8 +158,8 @@ def tile_picked_ykal_var_p_kernel(
         for h in range(2):
             nc.vector.tensor_tensor(resid[h][:], y_ps[h][:], mu[h], ALU.subtract)
         for h in range(2):
-            nc.vector.tensor_tensor(corr[h][:], resid[h][:], gain[h], ALU.mult)
-            nc.scalar.activation(widen[h][:], corr[h][:], ACT.Square, scale=math.sqrt(0.1))
+            nc.vector.scalar_tensor_tensor(corr[h][:], gain[h], 1.0, resid[h][:], ALU.add, ALU.mult)
+            nc.scalar.activation(widen[h][:], corr[h][:], ACT.Square, scale=math.sqrt(0.1) / 2)
         shrink = pool.tile([P, 2, HALF], F32, name="shrink", tag="resid0")
         for h in range(2):
             nc.vector.scalar_tensor_tensor(

@@ -40,8 +40,7 @@ def tile_picked_ykal_var_p_kernel(
         track_sb = pool.tile([P, S // LIST_ROWS], U16, name="track_sb")
         var_sb = pool.tile([P, U], F32, name="var_sb")
         words = [pool.tile([P, T], I32, name=f"words{o}") for o in range(PASSES)]
-        scales = late.tile([P, PASSES, T], U8, name="scales", offset=2048)
-        w1_raw = [late.tile([P, PACK, N], F32, name="w1_raw0", offset=0)]
+        scales = late.tile([P, PASSES, T], U8, name="scales", offset=1024)
         planes = pool.tile([P, PASSES, S], U8, name="planes", align_bytes=64)
         w2_raw = pool.tile([P, PASSES, PACK, N], F32, name="w2_raw")
 
@@ -64,7 +63,6 @@ def tile_picked_ykal_var_p_kernel(
         nc.sync.dma_start(w2_raw[:], w2.rearrange("(o p j) n -> p o j n", o=PASSES, j=PACK))
         load_words(0)
         load_words(1)
-        load_w1(0)
 
         halves = [slice(h * HALF, (h + 1) * HALF) for h in range(2)]
         list_halves = [slice(h * HALF // LIST_ROWS, (h + 1) * HALF // LIST_ROWS) for h in range(2)]
@@ -114,8 +112,9 @@ def tile_picked_ykal_var_p_kernel(
                 planes[j:P:QUADRANT].rearrange("p o s -> p (o s)").bitcast(I32),
                 picked_scales[4 + 8 * j : P : QUADRANT].rearrange("p o s -> p (o s)").bitcast(I32),
             )
-        w1_raw.append(late.tile([P, PACK, N], F32, name="w1_raw1", offset=2048))
+        w1_raw = [late.tile([P, PACK, N], F32, name=f"w1_raw{o}", offset=2048 * o) for o in range(PASSES)]
         mean_sb = late.tile([P, U], F32, name="mean_sb", offset=4096)
+        load_w1(0)
         load_w1(1)
         nc.sync.dma_start(mean_sb[:], mean)
         nc.vector.tensor_copy(ln_va[:], ln_var[:].indirect(track_sb[:]))
@@ -124,11 +123,12 @@ def tile_picked_ykal_var_p_kernel(
         nc.scalar.activation(va[:], ln_va[:], ACT.Exp, bias=-math.log(2.0))
         nc.vector.tensor_copy(picked_words[0][:], words[0][:].bitcast(U32).indirect(offs_sb[:]))
         for h in range(2):
+            product(z_ps, w2_mx[0], 0, h)
+        for h in range(2):
             nc.vector.tensor_copy(
                 picked_words[1][:, halves[h]], words[1][:].bitcast(U32).indirect(offs_sb[:, list_halves[h]])
             )
-            for o in range(PASSES):
-                product(z_ps, w2_mx[o], o, h)
+            product(z_ps, w2_mx[1], 1, h)
         w1_bf = [round_weights(w1_raw[o][:], f"w1_bf{o}") for o in range(PASSES)]
         w1_mx = [quantize(w1_bf[o], f"w1_mx{o}") for o in range(PASSES)]
 

@@ -52,9 +52,8 @@ def tile_picked_ykal_var_p_kernel(
             nc.sync.dma_start(w1_raw[o][:], rows.rearrange("(p j) n -> p j n", j=PACK))
 
         flat = scales[:].rearrange("p o t -> p (o t)").bitcast(I32)
-        nc.vector.memset(flat[:, :640], 0)
-        nc.gpsimd.memset(flat[:, 640:], 0)
-        nc.gpsimd.memset(planes[:].rearrange("p o s -> p (o s)").bitcast(I32), 0)
+        nc.vector.memset(flat, 0)
+        nc.vector.memset(planes[:].rearrange("p o s -> p (o s)").bitcast(I32), 0)
 
         nc.sync.dma_start(var_sb[:], var)
         nc.sync.dma_start(track_sb[:], track)

@@ -116,10 +116,12 @@ def tile_picked_ykal_var_p_kernel(
         load_w1(0)
         load_w1(1)
         nc.sync.dma_start(mean_sb[:], mean)
-        nc.vector.tensor_copy(ln_va[:], ln_var[:].indirect(track_sb[:]))
+        for h in range(2):
+            nc.vector.tensor_copy(ln_va[:, halves[h]], ln_var[:].indirect(track_sb[:, list_halves[h]]))
         w2_mx = [quantize(round_weights(w2_raw[:, o, :, :], f"w2_bf{o}"), f"w2_mx{o}") for o in range(PASSES)]
         va = new_tile("va", S, tag="w2_raw")
-        nc.scalar.activation(va[:], ln_va[:], ACT.Exp, bias=-math.log(2.0))
+        for h in range(2):
+            nc.scalar.activation(va[:, halves[h]], ln_va[:, halves[h]], ACT.Exp, bias=-math.log(2.0))
         nc.vector.tensor_copy(picked_words[0][:], words[0][:].bitcast(U32).indirect(offs_sb[:]))
         for h in range(2):
             product(z_ps, w2_mx[0], 0, h)

@@ -38,11 +38,11 @@ def tile_picked_ykal_var_p_kernel(
 
         offs_sb = pool.tile([P, S // LIST_ROWS], U16, name="offs_sb")
         track_sb = pool.tile([P, S // LIST_ROWS], U16, name="track_sb")
-        var_sb = pool.tile([P, U], F32, name="var_sb")
-        words = [pool.tile([P, T], I32, name=f"words{o}") for o in range(PASSES)]
-        scales = late.tile([P, PASSES, T], U8, name="scales", offset=1024)
-        planes = pool.tile([P, PASSES, S], U8, name="planes", align_bytes=64)
-        w2_raw = pool.tile([P, PASSES, PACK, N], F32, name="w2_raw")
+        var_sb = pool.tile([P, U], F32, name="var_sb", align_bytes=256)
+        words = [pool.tile([P, T], I32, name=f"words{o}", align_bytes=256) for o in range(PASSES)]
+        scales = late.tile([P, PASSES, T], U8, name="scales", offset=1024, align_bytes=256)
+        planes = pool.tile([P, PASSES, S], U8, name="planes", align_bytes=256)
+        w2_raw = pool.tile([P, PASSES, PACK, N], F32, name="w2_raw", align_bytes=256)
 
         def load_words(o):
             nc.sync.dma_start(words[o][:], x_words[o].rearrange("p t b -> p (t b)").bitcast(I32))
@@ -70,7 +70,7 @@ def tile_picked_ykal_var_p_kernel(
             return pool.tile([P, width], dtype, name=name, **options)
 
         ln_va = new_tile("ln_va", S)
-        picked_scales = pool.tile([P, PASSES, S], U8, name="picked_scales", align_bytes=64)
+        picked_scales = pool.tile([P, PASSES, S], U8, name="picked_scales", align_bytes=256)
         picked_words = [new_tile(f"picked_words{o}", S, U32, align_bytes=64) for o in range(PASSES)]
         z_ps = [psum.tile([P, HALF], F32, name=f"z_ps{h}") for h in range(2)]
         y_ps = [psum.tile([P, HALF], F32, name=f"y_ps{h}") for h in range(2)]
@@ -119,7 +119,7 @@ def tile_picked_ykal_var_p_kernel(
         for h in range(2):
             nc.vector.tensor_copy(ln_va[:, halves[h]], ln_var[:].indirect(track_sb[:, list_halves[h]]))
         w2_mx = [quantize(round_weights(w2_raw[:, o, :, :], f"w2_bf{o}"), f"w2_mx{o}") for o in range(PASSES)]
-        va = new_tile("va", S, tag="w2_raw")
+        va = new_tile("va", S, tag="w2_raw", align_bytes=256)
         for h in range(2):
             nc.scalar.activation(va[:, halves[h]], ln_va[:, halves[h]], ACT.Exp, bias=-math.log(2.0))
         nc.vector.tensor_copy(picked_words[0][:], words[0][:].bitcast(U32).indirect(offs_sb[:]))
@@ -155,7 +155,7 @@ def tile_picked_ykal_var_p_kernel(
         resid = [new_tile(f"resid{h}") for h in range(2)]
         corr = [new_tile(f"corr{h}") for h in range(2)]
         widen = [new_tile(f"widen{h}") for h in range(2)]
-        result = [new_tile(f"result{h}") for h in range(2)]
+        result = [new_tile(f"result{h}", align_bytes=256) for h in range(2)]
         for h in range(2):
             nc.vector.tensor_tensor(resid[h][:], y_ps[h][:], mu[h], ALU.subtract)
         for h in range(2):

@@ -75,12 +75,14 @@ def tile_picked_ykal_var_p_kernel(
         z_ps = [psum.tile([P, HALF], F32, name=f"z_ps{h}") for h in range(2)]
         y_ps = [psum.tile([P, HALF], F32, name=f"y_ps{h}") for h in range(2)]
 
-        def round_weights(raw, name):
+        def round_weights(raw, name, on_scalar=N):
             grouped = new_tile(name, N * PACK, BF16, align_bytes=64)
-            nc.scalar.copy(
-                grouped[:].rearrange("p (c i j) -> p c j i", i=RUN, j=PACK),
-                raw.rearrange("p j (c i) -> p c j i", i=RUN),
-            )
+            for copy, lo, hi in [(nc.scalar.copy, 0, on_scalar), (nc.vector.tensor_copy, on_scalar, N)]:
+                if lo < hi:
+                    copy(
+                        grouped[:, PACK * lo : PACK * hi].rearrange("p (c i j) -> p c j i", i=RUN, j=PACK),
+                        raw[:, :, lo:hi].rearrange("p j (c i) -> p c j i", i=RUN),
+                    )
             return grouped
 
         def quantize(grouped, name):
@@ -130,7 +132,7 @@ def tile_picked_ykal_var_p_kernel(
                 picked_words[1][:, halves[h]], words[1][:].bitcast(U32).indirect(offs_sb[:, list_halves[h]])
             )
             product(z_ps, w2_mx[1], 1, h)
-        w1_bf = [round_weights(w1_raw[o][:], f"w1_bf{o}") for o in range(PASSES)]
+        w1_bf = [round_weights(w1_raw[0][:], "w1_bf0"), round_weights(w1_raw[1][:], "w1_bf1", N - 32)]
         w1_mx = [quantize(w1_bf[o], f"w1_mx{o}") for o in range(PASSES)]
 
         gain0 = late.tile([P, HALF], F32, name="gain0", offset=2048)

@@ -23,8 +23,10 @@ PASSES = K // K_PASS
 QUADRANT = 32
 PLANE_ROWS = 4
 LIST_ROWS = 16
-HALF = S // 2
 RUN = 4
+HALF = S // 2
+PIECE = S // 4
+ON_VECTOR = 96
 
 
 def tile_picked_ykal_var_p_kernel(
@@ -36,23 +38,21 @@ def tile_picked_ykal_var_p_kernel(
         late = ctx.enter_context(tc.tile_pool(name="late", bufs=1))
         psum = ctx.enter_context(tc.psum_pool(name="psum", bufs=1))
 
-        offs_sb = pool.tile([P, S // LIST_ROWS], U16, name="offs_sb")
-        track_sb = pool.tile([P, S // LIST_ROWS], U16, name="track_sb")
-        var_sb = pool.tile([P, U], F32, name="var_sb", align_bytes=256)
-        words = [pool.tile([P, T], I32, name=f"words{o}", align_bytes=256) for o in range(PASSES)]
+        def new_tile(name, width, dtype=F32, **options):
+            return pool.tile([P, width], dtype, name=name, **options)
+
+        def entries(list_sb, lo, hi):
+            return list_sb[:, lo // LIST_ROWS : hi // LIST_ROWS]
+
+        offs_sb = new_tile("offs_sb", S // LIST_ROWS, U16)
+        track_sb = new_tile("track_sb", S // LIST_ROWS, U16)
+        var_sb = new_tile("var_sb", U, align_bytes=256)
+        words = [new_tile(f"words{o}", T, I32, align_bytes=256) for o in range(PASSES)]
         scales = late.tile([P, PASSES, T], U8, name="scales", offset=1024, align_bytes=256)
         planes = pool.tile([P, PASSES, S], U8, name="planes", align_bytes=256)
         w2_raw = pool.tile([P, PASSES, PACK, N], F32, name="w2_raw", align_bytes=256)
 
-        def load_words(o):
-            nc.sync.dma_start(words[o][:], x_words[o].rearrange("p t b -> p (t b)").bitcast(I32))
-
-        def load_w1(o):
-            rows = w1[K_PASS * o : K_PASS * (o + 1), :]
-            nc.sync.dma_start(w1_raw[o][:], rows.rearrange("(p j) n -> p j n", j=PACK))
-
-        flat = scales[:].rearrange("p o t -> p (o t)").bitcast(I32)
-        nc.vector.memset(flat, 0)
+        nc.vector.memset(scales[:].rearrange("p o t -> p (o t)").bitcast(I32), 0)
         nc.vector.memset(planes[:].rearrange("p o s -> p (o s)").bitcast(I32), 0)
 
         nc.sync.dma_start(var_sb[:], var)
@@ -60,52 +60,10 @@ def tile_picked_ykal_var_p_kernel(
         nc.sync.dma_start(offs_sb[:], offs)
         nc.sync.dma_start(scales[4:P:8, :, :].bitcast(I32), x_scales.rearrange("o r t -> r o t").bitcast(I32))
         nc.sync.dma_start(w2_raw[:], w2.rearrange("(o p j) n -> p o j n", o=PASSES, j=PACK))
-        load_words(0)
-        load_words(1)
+        for o in range(PASSES):
+            nc.sync.dma_start(words[o][:], x_words[o].rearrange("p t b -> p (t b)").bitcast(I32))
 
-        halves = [slice(h * HALF, (h + 1) * HALF) for h in range(2)]
-        list_halves = [slice(h * HALF // LIST_ROWS, (h + 1) * HALF // LIST_ROWS) for h in range(2)]
-
-        def new_tile(name, width=HALF, dtype=F32, **options):
-            return pool.tile([P, width], dtype, name=name, **options)
-
-        ln_va = new_tile("ln_va", S)
         picked_scales = pool.tile([P, PASSES, S], U8, name="picked_scales", align_bytes=256)
-        picked_words = [new_tile(f"picked_words{o}", S, U32, align_bytes=64) for o in range(PASSES)]
-        z_ps = [psum.tile([P, HALF], F32, name=f"z_ps{h}") for h in range(2)]
-        y_ps = [psum.tile([P, HALF], F32, name=f"y_ps{h}") for h in range(2)]
-
-        def round_weights(raw, name, on_scalar=N):
-            grouped = new_tile(name, N * PACK, BF16, align_bytes=64)
-            for copy, lo, hi in [(nc.scalar.copy, 0, on_scalar), (nc.vector.tensor_copy, on_scalar, N)]:
-                if lo < hi:
-                    copy(
-                        grouped[:, PACK * lo : PACK * hi].rearrange("p (c i j) -> p c j i", i=RUN, j=PACK),
-                        raw[:, :, lo:hi].rearrange("p j (c i) -> p c j i", i=RUN),
-                    )
-            return grouped
-
-        def quantize(grouped, name):
-            codes = new_tile(name + "_codes", N, U32, align_bytes=64)
-            plane = new_tile(name + "_plane", N, U8, align_bytes=64)
-            nc.vector.quantize_mx(out=codes[:].bitcast(FP8X4), scales=plane[:], in_=grouped[:])
-            return codes, plane
-
-        def product(acc, weight, o, h):
-            codes, plane = weight
-            nc.tensor.matmul_mx(
-                out=acc[h][:],
-                lhsT=codes[:].bitcast(FP8X4),
-                lhsT_scale=plane[:],
-                rhs=picked_words[o][:, halves[h]].bitcast(FP8X4),
-                rhs_scale=planes[:, o, halves[h]],
-                start=(o == 0),
-                stop=(o == PASSES - 1),
-            )
-
-        ln_var = new_tile("ln_var", U)
-        nc.scalar.activation(ln_var[:], var_sb[:], ACT.Ln)
-
         for o in range(PASSES):
             nc.vector.tensor_copy(picked_scales[:, o, :], scales[:, o, :].indirect(offs_sb[:]))
         for j in range(PLANE_ROWS):
@@ -115,59 +73,103 @@ def tile_picked_ykal_var_p_kernel(
             )
         w1_raw = [late.tile([P, PACK, N], F32, name=f"w1_raw{o}", offset=2048 * o) for o in range(PASSES)]
         mean_sb = late.tile([P, U], F32, name="mean_sb", offset=4096)
-        load_w1(0)
-        load_w1(1)
+        for o in range(PASSES):
+            nc.sync.dma_start(w1_raw[o][:], w1[K_PASS * o : K_PASS * (o + 1), :].rearrange("(p j) n -> p j n", j=PACK))
         nc.sync.dma_start(mean_sb[:], mean)
-        for h in range(2):
-            nc.vector.tensor_copy(ln_va[:, halves[h]], ln_var[:].indirect(track_sb[:, list_halves[h]]))
-        w2_mx = [quantize(round_weights(w2_raw[:, o, :, :], f"w2_bf{o}"), f"w2_mx{o}") for o in range(PASSES)]
-        va = new_tile("va", S, tag="w2_raw", align_bytes=256)
-        for h in range(2):
-            nc.scalar.activation(va[:, halves[h]], ln_va[:, halves[h]], ACT.Exp, bias=-math.log(2.0))
+
+        ln_var = new_tile("ln_var", U)
+        ln_va = new_tile("ln_va", S)
+        half_va = new_tile("half_va", S)
+        nc.scalar.activation(ln_var[:], var_sb[:], ACT.Ln)
+        nc.scalar.activation(ln_va[:], ln_var[:].indirect(track_sb[:]), ACT.Copy)
+        nc.scalar.activation(half_va[:], ln_va[:], ACT.Exp, bias=-math.log(2.0))
+
+        def quantize(grouped, name, width):
+            codes = new_tile(name + "_codes", width, U32, align_bytes=64)
+            plane = new_tile(name + "_plane", width, U8, align_bytes=64)
+            nc.vector.quantize_mx(out=codes[:].bitcast(FP8X4), scales=plane[:], in_=grouped[:])
+            return codes, plane
+
+        w2_bf = new_tile("w2_bf", PASSES * N * PACK, BF16, align_bytes=64)
+        nc.vector.tensor_copy(
+            w2_bf[:].rearrange("p (o c i j) -> p o c j i", o=PASSES, i=RUN, j=PACK),
+            w2_raw[:].rearrange("p o j (c i) -> p o c j i", i=RUN),
+        )
+        w2_codes, w2_plane = quantize(w2_bf, "w2", PASSES * N)
+        w2_mx = [(w2_codes[:, N * o : N * (o + 1)], w2_plane[:, N * o : N * (o + 1)]) for o in range(PASSES)]
+
+        picked_words = [new_tile(f"picked_words{o}", S, U32, align_bytes=64) for o in range(PASSES)]
+        z_ps = [psum.tile([P, HALF], F32, name=f"z_ps{h}") for h in range(2)]
+        y_ps = [psum.tile([P, HALF], F32, name=f"y_ps{h}") for h in range(2)]
+
+        def product(acc, weight, o, h):
+            codes, plane = weight
+            cols = slice(h * HALF, (h + 1) * HALF)
+            nc.tensor.matmul_mx(
+                out=acc[h][:],
+                lhsT=codes.bitcast(FP8X4),
+                lhsT_scale=plane,
+                rhs=picked_words[o][:, cols].bitcast(FP8X4),
+                rhs_scale=planes[:, o, cols],
+                start=(o == 0),
+                stop=(o == PASSES - 1),
+            )
+
         nc.vector.tensor_copy(picked_words[0][:], words[0][:].bitcast(U32).indirect(offs_sb[:]))
         for h in range(2):
             product(z_ps, w2_mx[0], 0, h)
         for h in range(2):
-            nc.vector.tensor_copy(
-                picked_words[1][:, halves[h]], words[1][:].bitcast(U32).indirect(offs_sb[:, list_halves[h]])
-            )
+            lo, hi = h * HALF, (h + 1) * HALF
+            nc.vector.tensor_copy(picked_words[1][:, lo:hi], words[1][:].bitcast(U32).indirect(entries(offs_sb, lo, hi)))
             product(z_ps, w2_mx[1], 1, h)
-        w1_bf = [round_weights(w1_raw[0][:], "w1_bf0"), round_weights(w1_raw[1][:], "w1_bf1", N - 32)]
-        w1_mx = [quantize(w1_bf[o], f"w1_mx{o}") for o in range(PASSES)]
 
-        gain0 = late.tile([P, HALF], F32, name="gain0", offset=2048)
-        z1 = late.tile([P, HALF], F32, name="z1", offset=3072)
-        logit0 = late.tile([P, HALF], F32, name="logit0", offset=0)
-        logit = [logit0[:], new_tile("logit1")[:]]
-        gain = [gain0[:], new_tile("gain1")[:]]
-        mu = [new_tile("mu0")[:], new_tile("mu1")[:]]
-        z1_sb = z1[:]
+        def round_w1(o, on_vector):
+            grouped = new_tile(f"w1_bf{o}", N * PACK, BF16, align_bytes=64)
+            split = N - on_vector
+            for copy, lo, hi in [(nc.scalar.copy, 0, split), (nc.vector.tensor_copy, split, N)]:
+                if lo < hi:
+                    copy(
+                        grouped[:, PACK * lo : PACK * hi].rearrange("p (c i j) -> p c j i", i=RUN, j=PACK),
+                        w1_raw[o][:, :, lo:hi].rearrange("p j (c i) -> p c j i", i=RUN),
+                    )
+            return grouped
 
-        nc.vector.tensor_tensor(logit[0], ln_va[:, halves[0]], z_ps[0][:], ALU.subtract)
-        nc.scalar.copy(z1_sb, z_ps[1][:])
-        nc.gpsimd.tensor_tensor(logit[1], ln_va[:, halves[1]], z1_sb, ALU.subtract)
+        w1_bf = [round_w1(0, 0), round_w1(1, ON_VECTOR)]
+        logit = [late.tile([P, HALF], F32, name=f"logit{h}", offset=2048 * h) for h in range(2)]
+        tanh0 = late.tile([P, HALF], F32, name="tanh0", offset=3072)
+        halves = [slice(h * HALF, (h + 1) * HALF) for h in range(2)]
+        w1_mx = []
         for h in range(2):
-            nc.scalar.activation(gain[h], logit[h], ACT.Tanh, scale=0.5)
+            codes, plane = quantize(w1_bf[h], f"w1_{h}", N)
+            w1_mx.append((codes[:], plane[:]))
+            nc.vector.tensor_tensor(logit[h][:], ln_va[:, halves[h]], z_ps[h][:], ALU.subtract)
         for o in range(PASSES):
             for h in range(2):
                 product(y_ps, w1_mx[o], o, h)
 
+        mu = [new_tile(f"mu{h}", HALF) for h in range(2)]
+        resid = [new_tile(f"resid{h}", HALF) for h in range(2)]
+        widen = [new_tile(f"widen{h}", HALF) for h in range(2)]
+        result = [new_tile(f"result{h}", HALF, align_bytes=256) for h in range(2)]
+
+        nc.scalar.activation(tanh0[:], logit[0][:], ACT.Tanh, scale=0.5)
+        nc.scalar.activation(mu[1][:], mean_sb[:].indirect(entries(track_sb, HALF, S)), ACT.Copy)
+        for lo in (0, PIECE):
+            nc.vector.tensor_copy(mu[0][:, lo : lo + PIECE], mean_sb[:].indirect(entries(track_sb, lo, lo + PIECE)))
+        tanh1 = late.tile([P, HALF], F32, name="tanh1", offset=4096)
+        tanh = [tanh0, tanh1]
+        nc.scalar.activation(tanh1[:], logit[1][:], ACT.Tanh, scale=0.5)
+        for lo in (0, PIECE):
+            cols = slice(lo, lo + PIECE)
+            nc.vector.tensor_tensor(resid[0][:, cols], y_ps[0][:, cols], mu[0][:, cols], ALU.subtract)
+        nc.vector.tensor_tensor(resid[1][:], y_ps[1][:], mu[1][:], ALU.subtract)
+        corr = [late.tile([P, HALF], F32, name="corr0", offset=2048), new_tile("corr1", HALF)]
         for h in range(2):
-            nc.vector.tensor_copy(mu[h], mean_sb[:].indirect(track_sb[:, list_halves[h]]))
-        resid = [new_tile(f"resid{h}") for h in range(2)]
-        corr = [new_tile(f"corr{h}") for h in range(2)]
-        widen = [new_tile(f"widen{h}") for h in range(2)]
-        result = [new_tile(f"result{h}", align_bytes=256) for h in range(2)]
-        for h in range(2):
-            nc.vector.tensor_tensor(resid[h][:], y_ps[h][:], mu[h], ALU.subtract)
-        for h in range(2):
-            nc.vector.scalar_tensor_tensor(corr[h][:], gain[h], 1.0, resid[h][:], ALU.add, ALU.mult)
+            nc.vector.scalar_tensor_tensor(corr[h][:], tanh[h][:], 1.0, resid[h][:], ALU.add, ALU.mult)
             nc.scalar.activation(widen[h][:], corr[h][:], ACT.Square, scale=math.sqrt(0.1) / 2)
         shrink = pool.tile([P, 2, HALF], F32, name="shrink", tag="resid0")
         for h in range(2):
-            nc.vector.scalar_tensor_tensor(
-                shrink[:, h, :], gain[h], 1.0, va[:, halves[h]], ALU.subtract, ALU.mult
-            )
+            nc.vector.scalar_tensor_tensor(shrink[:, h, :], tanh[h][:], 1.0, half_va[:, halves[h]], ALU.subtract, ALU.mult)
         for h in range(2):
             nc.vector.tensor_tensor(result[h][:], widen[h][:], shrink[:, h, :], ALU.subtract)
             nc.sync.dma_start(out[:, halves[h]], result[h][:])

@@ -26,7 +26,7 @@ LIST_ROWS = 16
 RUN = 4
 HALF = S // 2
 PIECE = S // 4
-ON_VECTOR = 96
+ON_VECTOR = 32
 
 
 def tile_picked_ykal_var_p_kernel(
@@ -163,7 +163,7 @@ def tile_picked_ykal_var_p_kernel(
             cols = slice(lo, lo + PIECE)
             nc.vector.tensor_tensor(resid[0][:, cols], y_ps[0][:, cols], mu[0][:, cols], ALU.subtract)
         nc.vector.tensor_tensor(resid[1][:], y_ps[1][:], mu[1][:], ALU.subtract)
-        corr = [late.tile([P, HALF], F32, name="corr0", offset=2048), new_tile("corr1", HALF)]
+        corr = [late.tile([P, HALF], F32, name="corr0", offset=5120), new_tile("corr1", HALF)]
         for h in range(2):
             nc.vector.scalar_tensor_tensor(corr[h][:], tanh[h][:], 1.0, resid[h][:], ALU.add, ALU.mult)
             nc.scalar.activation(widen[h][:], corr[h][:], ACT.Square, scale=math.sqrt(0.1) / 2)

@@ -48,17 +48,16 @@ def tile_picked_ykal_var_p_kernel(
         track_sb = new_tile("track_sb", S // LIST_ROWS, U16)
         var_sb = new_tile("var_sb", U, align_bytes=256)
         words = [new_tile(f"words{o}", T, I32, align_bytes=256) for o in range(PASSES)]
-        scales = late.tile([P, PASSES, T], U8, name="scales", offset=1024, align_bytes=256)
+        scales = pool.tile([P, PASSES, T], U8, name="scales", align_bytes=256)
         planes = pool.tile([P, PASSES, S], U8, name="planes", align_bytes=256)
         w2_raw = pool.tile([P, PASSES, PACK, N], F32, name="w2_raw", align_bytes=256)
 
         nc.vector.memset(scales[:].rearrange("p o t -> p (o t)").bitcast(I32), 0)
-        nc.vector.memset(planes[:].rearrange("p o s -> p (o s)").bitcast(I32), 0)
 
         nc.sync.dma_start(var_sb[:], var)
         nc.sync.dma_start(track_sb[:], track)
         nc.sync.dma_start(offs_sb[:], offs)
-        nc.sync.dma_start(scales[4:P:8, :, :].bitcast(I32), x_scales.rearrange("o r t -> r o t").bitcast(I32))
+        nc.sync.dma_start(scales[0:P:8, :, :].bitcast(I32), x_scales.rearrange("o r t -> r o t").bitcast(I32))
         nc.sync.dma_start(w2_raw[:], w2.rearrange("(o p j) n -> p o j n", o=PASSES, j=PACK))
         for o in range(PASSES):
             nc.sync.dma_start(words[o][:], x_words[o].rearrange("p t b -> p (t b)").bitcast(I32))
@@ -66,23 +65,20 @@ def tile_picked_ykal_var_p_kernel(
         picked_scales = pool.tile([P, PASSES, S], U8, name="picked_scales", align_bytes=256)
         for o in range(PASSES):
             nc.vector.tensor_copy(picked_scales[:, o, :], scales[:, o, :].indirect(offs_sb[:]))
-        for j in range(PLANE_ROWS):
+        nc.vector.tensor_copy(
+            planes[:].rearrange("p o s -> p (o s)").bitcast(I32), picked_scales[:].rearrange("p o s -> p (o s)").bitcast(I32)
+        )
+        for j in range(1, PLANE_ROWS):
             nc.sync.dma_start(
                 planes[j:P:QUADRANT].rearrange("p o s -> p (o s)").bitcast(I32),
-                picked_scales[4 + 8 * j : P : QUADRANT].rearrange("p o s -> p (o s)").bitcast(I32),
+                picked_scales[8 * j : P : QUADRANT].rearrange("p o s -> p (o s)").bitcast(I32),
             )
-        w1_raw = [late.tile([P, PACK, N], F32, name=f"w1_raw{o}", offset=2048 * o) for o in range(PASSES)]
-        mean_sb = late.tile([P, U], F32, name="mean_sb", offset=4096)
-        for o in range(PASSES):
-            nc.sync.dma_start(w1_raw[o][:], w1[K_PASS * o : K_PASS * (o + 1), :].rearrange("(p j) n -> p j n", j=PACK))
-        nc.sync.dma_start(mean_sb[:], mean)
-
-        ln_var = new_tile("ln_var", U)
+        ln_var = late.tile([P, U], F32, name="ln_var", offset=1024)
         ln_va = new_tile("ln_va", S)
-        half_va = new_tile("half_va", S)
+        va = new_tile("va", S)
         nc.scalar.activation(ln_var[:], var_sb[:], ACT.Ln)
         nc.scalar.activation(ln_va[:], ln_var[:].indirect(track_sb[:]), ACT.Copy)
-        nc.scalar.activation(half_va[:], ln_va[:], ACT.Exp, bias=-math.log(2.0))
+        nc.scalar.activation(va[:], ln_va[:], ACT.Exp)
 
         def quantize(grouped, name, width):
             codes = new_tile(name + "_codes", width, U32, align_bytes=64)
@@ -95,6 +91,12 @@ def tile_picked_ykal_var_p_kernel(
             w2_bf[:].rearrange("p (o c i j) -> p o c j i", o=PASSES, i=RUN, j=PACK),
             w2_raw[:].rearrange("p o j (c i) -> p o c j i", i=RUN),
         )
+        w1_raw = [late.tile([P, PACK, N], F32, name=f"w1_raw{o}", offset=2048 * o) for o in range(PASSES)]
+        mean_sb = late.tile([P, U], F32, name="mean_sb", offset=4096)
+        for o in range(PASSES):
+            nc.sync.dma_start(w1_raw[o][:], w1[K_PASS * o : K_PASS * (o + 1), :].rearrange("(p j) n -> p j n", j=PACK))
+        nc.sync.dma_start(mean_sb[:], mean)
+
         w2_codes, w2_plane = quantize(w2_bf, "w2", PASSES * N)
         w2_mx = [(w2_codes[:, N * o : N * (o + 1)], w2_plane[:, N * o : N * (o + 1)]) for o in range(PASSES)]
 
@@ -169,7 +171,7 @@ def tile_picked_ykal_var_p_kernel(
             nc.scalar.activation(widen[h][:], corr[h][:], ACT.Square, scale=math.sqrt(0.1) / 2)
         shrink = pool.tile([P, 2, HALF], F32, name="shrink", tag="resid0")
         for h in range(2):
-            nc.vector.scalar_tensor_tensor(shrink[:, h, :], tanh[h][:], 1.0, half_va[:, halves[h]], ALU.subtract, ALU.mult)
+            nc.vector.scalar_tensor_tensor(shrink[:, h, :], tanh[h][:], 1.0, va[:, halves[h]], ALU.subtract, ALU.mult)
         for h in range(2):
-            nc.vector.tensor_tensor(result[h][:], widen[h][:], shrink[:, h, :], ALU.subtract)
+            nc.vector.scalar_tensor_tensor(result[h][:], shrink[:, h, :], -0.5, widen[h][:], ALU.mult, ALU.add)
             nc.sync.dma_start(out[:, halves[h]], result[h][:])

@@ -26,7 +26,8 @@ LIST_ROWS = 16
 RUN = 4
 HALF = S // 2
 PIECE = S // 4
-ON_VECTOR = 32
+ON_GPSIMD = 32
+ON_VECTOR = 48
 
 
 def tile_picked_ykal_var_p_kernel(
@@ -104,39 +105,40 @@ def tile_picked_ykal_var_p_kernel(
         z_ps = [psum.tile([P, HALF], F32, name=f"z_ps{h}") for h in range(2)]
         y_ps = [psum.tile([P, HALF], F32, name=f"y_ps{h}") for h in range(2)]
 
-        def product(acc, weight, o, h):
+        def product(acc, weight, o, h, lo=0, hi=HALF):
             codes, plane = weight
-            cols = slice(h * HALF, (h + 1) * HALF)
+            cols = slice(h * HALF + lo, h * HALF + hi)
             nc.tensor.matmul_mx(
-                out=acc[h][:],
+                out=acc[h][:, lo:hi],
                 lhsT=codes.bitcast(FP8X4),
                 lhsT_scale=plane,
                 rhs=picked_words[o][:, cols].bitcast(FP8X4),
                 rhs_scale=planes[:, o, cols],
                 start=(o == 0),
-                stop=(o == PASSES - 1),
+                stop=(o == PASSES - 1 and hi == HALF),
             )
 
         nc.vector.tensor_copy(picked_words[0][:], words[0][:].bitcast(U32).indirect(offs_sb[:]))
         for h in range(2):
             product(z_ps, w2_mx[0], 0, h)
-        for h in range(2):
-            lo, hi = h * HALF, (h + 1) * HALF
-            nc.vector.tensor_copy(picked_words[1][:, lo:hi], words[1][:].bitcast(U32).indirect(entries(offs_sb, lo, hi)))
-            product(z_ps, w2_mx[1], 1, h)
+        for h, lo, hi in [(0, 0, HALF), (1, 0, PIECE), (1, PIECE, HALF)]:
+            first, last = h * HALF + lo, h * HALF + hi
+            nc.vector.tensor_copy(
+                picked_words[1][:, first:last], words[1][:].bitcast(U32).indirect(entries(offs_sb, first, last))
+            )
+            product(z_ps, w2_mx[1], 1, h, lo, hi)
 
-        def round_w1(o, on_vector):
-            grouped = new_tile(f"w1_bf{o}", N * PACK, BF16, align_bytes=64)
-            split = N - on_vector
-            for copy, lo, hi in [(nc.scalar.copy, 0, split), (nc.vector.tensor_copy, split, N)]:
-                if lo < hi:
-                    copy(
-                        grouped[:, PACK * lo : PACK * hi].rearrange("p (c i j) -> p c j i", i=RUN, j=PACK),
-                        w1_raw[o][:, :, lo:hi].rearrange("p j (c i) -> p c j i", i=RUN),
-                    )
-            return grouped
+        def rounding_views(o, grouped, lo, hi):
+            return (
+                grouped[:, PACK * lo : PACK * hi].rearrange("p (c i j) -> p c j i", i=RUN, j=PACK),
+                w1_raw[o][:, :, lo:hi].rearrange("p j (c i) -> p c j i", i=RUN),
+            )
 
-        w1_bf = [round_w1(0, 0), round_w1(1, ON_VECTOR)]
+        w1_bf = [new_tile(f"w1_bf{o}", N * PACK, BF16, align_bytes=64) for o in range(PASSES)]
+        nc.scalar.copy(*rounding_views(0, w1_bf[0], 0, N - ON_GPSIMD))
+        nc.gpsimd.tensor_scalar(*rounding_views(0, w1_bf[0], N - ON_GPSIMD, N), 1.0, 0.0, ALU.mult, ALU.add)
+        nc.scalar.copy(*rounding_views(1, w1_bf[1], 0, N - ON_VECTOR))
+        nc.vector.tensor_copy(*rounding_views(1, w1_bf[1], N - ON_VECTOR, N))
         logit = [late.tile([P, HALF], F32, name=f"logit{h}", offset=2048 * h) for h in range(2)]
         tanh0 = late.tile([P, HALF], F32, name="tanh0", offset=3072)
         halves = [slice(h * HALF, (h + 1) * HALF) for h in range(2)]

@@ -102,31 +102,31 @@ def tile_picked_ykal_var_p_kernel(
         w2_mx = [(w2_codes[:, N * o : N * (o + 1)], w2_plane[:, N * o : N * (o + 1)]) for o in range(PASSES)]
 
         picked_words = [new_tile(f"picked_words{o}", S, U32, align_bytes=64) for o in range(PASSES)]
-        z_ps = [psum.tile([P, HALF], F32, name=f"z_ps{h}") for h in range(2)]
+        z_cols = [slice(0, HALF), slice(HALF, HALF + PIECE), slice(HALF + PIECE, S)]
+        z_ps = [psum.tile([P, cols.stop - cols.start], F32, name=f"z_ps{i}") for i, cols in enumerate(z_cols)]
         y_ps = [psum.tile([P, HALF], F32, name=f"y_ps{h}") for h in range(2)]
 
-        def product(acc, weight, o, h, lo=0, hi=HALF):
+        def product(acc, weight, o, cols):
             codes, plane = weight
-            cols = slice(h * HALF + lo, h * HALF + hi)
             nc.tensor.matmul_mx(
-                out=acc[h][:, lo:hi],
+                out=acc[:],
                 lhsT=codes.bitcast(FP8X4),
                 lhsT_scale=plane,
                 rhs=picked_words[o][:, cols].bitcast(FP8X4),
                 rhs_scale=planes[:, o, cols],
                 start=(o == 0),
-                stop=(o == PASSES - 1 and hi == HALF),
+                stop=(o == PASSES - 1),
             )
 
         nc.vector.tensor_copy(picked_words[0][:], words[0][:].bitcast(U32).indirect(offs_sb[:]))
-        for h in range(2):
-            product(z_ps, w2_mx[0], 0, h)
-        for h, lo, hi in [(0, 0, HALF), (1, 0, PIECE), (1, PIECE, HALF)]:
-            first, last = h * HALF + lo, h * HALF + hi
+        for cols in z_cols:
             nc.vector.tensor_copy(
-                picked_words[1][:, first:last], words[1][:].bitcast(U32).indirect(entries(offs_sb, first, last))
+                picked_words[1][:, cols], words[1][:].bitcast(U32).indirect(entries(offs_sb, cols.start, cols.stop))
             )
-            product(z_ps, w2_mx[1], 1, h, lo, hi)
+        for pieces in ([0], [1, 2]):
+            for o in range(PASSES):
+                for i in pieces:
+                    product(z_ps[i], w2_mx[o], o, z_cols[i])
 
         def rounding_views(o, grouped, lo, hi):
             return (
@@ -143,13 +143,16 @@ def tile_picked_ykal_var_p_kernel(
         tanh0 = late.tile([P, HALF], F32, name="tanh0", offset=3072)
         halves = [slice(h * HALF, (h + 1) * HALF) for h in range(2)]
         w1_mx = []
-        for h in range(2):
-            codes, plane = quantize(w1_bf[h], f"w1_{h}", N)
+        for o in range(PASSES):
+            codes, plane = quantize(w1_bf[o], f"w1_{o}", N)
             w1_mx.append((codes[:], plane[:]))
-            nc.vector.tensor_tensor(logit[h][:], ln_va[:, halves[h]], z_ps[h][:], ALU.subtract)
+            if o == 0:
+                nc.vector.tensor_tensor(logit[0][:], ln_va[:, z_cols[0]], z_ps[0][:], ALU.subtract)
+        nc.vector.tensor_tensor(logit[1][:, :PIECE], ln_va[:, z_cols[1]], z_ps[1][:], ALU.subtract)
+        nc.vector.tensor_tensor(logit[1][:, PIECE:], ln_va[:, z_cols[2]], z_ps[2][:], ALU.subtract)
         for o in range(PASSES):
             for h in range(2):
-                product(y_ps, w1_mx[o], o, h)
+                product(y_ps[h], w1_mx[o], o, halves[h])
 
         mu = [new_tile(f"mu{h}", HALF) for h in range(2)]
         resid = [new_tile(f"resid{h}", HALF) for h in range(2)]

@@ -103,8 +103,10 @@ def tile_picked_ykal_var_p_kernel(
 
         picked_words = [new_tile(f"picked_words{o}", S, U32, align_bytes=64) for o in range(PASSES)]
         z_cols = [slice(0, HALF), slice(HALF, HALF + PIECE), slice(HALF + PIECE, S)]
+        quarters = [slice(q * PIECE, (q + 1) * PIECE) for q in range(4)]
+        halves = [slice(h * HALF, (h + 1) * HALF) for h in range(2)]
         z_ps = [psum.tile([P, cols.stop - cols.start], F32, name=f"z_ps{i}") for i, cols in enumerate(z_cols)]
-        y_ps = [psum.tile([P, HALF], F32, name=f"y_ps{h}") for h in range(2)]
+        y_ps = [psum.tile([P, PIECE], F32, name=f"y_ps{q}") for q in range(4)]
 
         def product(acc, weight, o, cols):
             codes, plane = weight
@@ -141,7 +143,6 @@ def tile_picked_ykal_var_p_kernel(
         nc.vector.tensor_copy(*rounding_views(1, w1_bf[1], N - ON_VECTOR, N))
         logit = [late.tile([P, HALF], F32, name=f"logit{h}", offset=2048 * h) for h in range(2)]
         tanh0 = late.tile([P, HALF], F32, name="tanh0", offset=3072)
-        halves = [slice(h * HALF, (h + 1) * HALF) for h in range(2)]
         w1_mx = []
         for o in range(PASSES):
             codes, plane = quantize(w1_bf[o], f"w1_{o}", N)
@@ -151,32 +152,40 @@ def tile_picked_ykal_var_p_kernel(
         nc.vector.tensor_tensor(logit[1][:, :PIECE], ln_va[:, z_cols[1]], z_ps[1][:], ALU.subtract)
         nc.vector.tensor_tensor(logit[1][:, PIECE:], ln_va[:, z_cols[2]], z_ps[2][:], ALU.subtract)
         for o in range(PASSES):
-            for h in range(2):
-                product(y_ps[h], w1_mx[o], o, halves[h])
+            for q in range(4):
+                product(y_ps[q], w1_mx[o], o, quarters[q])
 
-        mu = [new_tile(f"mu{h}", HALF) for h in range(2)]
-        resid = [new_tile(f"resid{h}", HALF) for h in range(2)]
-        widen = [new_tile(f"widen{h}", HALF) for h in range(2)]
+        mu = [new_tile(f"mu{q}", PIECE) for q in range(4)]
+        resid = [new_tile(f"resid{q}", PIECE) for q in range(4)]
+        corr = [new_tile(f"corr{q}", PIECE) for q in range(4)]
+        widen = [new_tile(f"widen{q}", PIECE) for q in range(4)]
         result = [new_tile(f"result{h}", HALF, align_bytes=256) for h in range(2)]
 
         nc.scalar.activation(tanh0[:], logit[0][:], ACT.Tanh, scale=0.5)
-        nc.scalar.activation(mu[1][:], mean_sb[:].indirect(entries(track_sb, HALF, S)), ACT.Copy)
-        for lo in (0, PIECE):
-            nc.vector.tensor_copy(mu[0][:, lo : lo + PIECE], mean_sb[:].indirect(entries(track_sb, lo, lo + PIECE)))
-        tanh1 = late.tile([P, HALF], F32, name="tanh1", offset=4096)
-        tanh = [tanh0, tanh1]
+        shrink0 = new_tile("shrink0", HALF)
+        nc.vector.scalar_tensor_tensor(shrink0[:], tanh0[:], 1.0, va[:, halves[0]], ALU.subtract, ALU.mult)
+        for q in range(4):
+            picked_mean = mean_sb[:].indirect(entries(track_sb, q * PIECE, (q + 1) * PIECE))
+            if q == 0:
+                nc.vector.tensor_copy(mu[q][:], picked_mean)
+            else:
+                nc.scalar.activation(mu[q][:], picked_mean, ACT.Copy)
+        tanh1 = new_tile("tanh1", HALF)
         nc.scalar.activation(tanh1[:], logit[1][:], ACT.Tanh, scale=0.5)
-        for lo in (0, PIECE):
-            cols = slice(lo, lo + PIECE)
-            nc.vector.tensor_tensor(resid[0][:, cols], y_ps[0][:, cols], mu[0][:, cols], ALU.subtract)
-        nc.vector.tensor_tensor(resid[1][:], y_ps[1][:], mu[1][:], ALU.subtract)
-        corr = [late.tile([P, HALF], F32, name="corr0", offset=5120), new_tile("corr1", HALF)]
-        for h in range(2):
-            nc.vector.scalar_tensor_tensor(corr[h][:], tanh[h][:], 1.0, resid[h][:], ALU.add, ALU.mult)
-            nc.scalar.activation(widen[h][:], corr[h][:], ACT.Square, scale=math.sqrt(0.1) / 2)
-        shrink = pool.tile([P, 2, HALF], F32, name="shrink", tag="resid0")
-        for h in range(2):
-            nc.vector.scalar_tensor_tensor(shrink[:, h, :], tanh[h][:], 1.0, va[:, halves[h]], ALU.subtract, ALU.mult)
-        for h in range(2):
-            nc.vector.scalar_tensor_tensor(result[h][:], shrink[:, h, :], -0.5, widen[h][:], ALU.mult, ALU.add)
-            nc.sync.dma_start(out[:, halves[h]], result[h][:])
+        tanh = [(tanh0, tanh1)[q // 2][:, quarters[q % 2]] for q in range(4)]
+        for q in range(4):
+            nc.vector.tensor_tensor(resid[q][:], y_ps[q][:], mu[q][:], ALU.subtract)
+        for q in range(4):
+            nc.vector.scalar_tensor_tensor(corr[q][:], tanh[q], 1.0, resid[q][:], ALU.add, ALU.mult)
+            nc.scalar.activation(widen[q][:], corr[q][:], ACT.Square, scale=math.sqrt(0.1) / 2)
+        shrink = [shrink0[:, quarters[0]], shrink0[:, quarters[1]]]
+        for q in (2, 3):
+            kept = new_tile(f"shrink{q}", PIECE)
+            nc.vector.scalar_tensor_tensor(kept[:], tanh[q], 1.0, va[:, quarters[q]], ALU.subtract, ALU.mult)
+            shrink.append(kept[:])
+        for q in range(4):
+            nc.vector.scalar_tensor_tensor(
+                result[q // 2][:, quarters[q % 2]], shrink[q], -0.5, widen[q][:], ALU.mult, ALU.add
+            )
+            if q % 2 == 1:
+                nc.sync.dma_start(out[:, halves[q // 2]], result[q // 2][:])

@@ -155,7 +155,7 @@ def tile_picked_ykal_var_p_kernel(
             for q in range(4):
                 product(y_ps[q], w1_mx[o], o, quarters[q])
 
-        mu = [new_tile(f"mu{q}", PIECE) for q in range(4)]
+        mu = new_tile("mu", S)
         resid = [new_tile(f"resid{q}", PIECE) for q in range(4)]
         corr = [new_tile(f"corr{q}", PIECE) for q in range(4)]
         widen = [new_tile(f"widen{q}", PIECE) for q in range(4)]
@@ -164,17 +164,15 @@ def tile_picked_ykal_var_p_kernel(
         nc.scalar.activation(tanh0[:], logit[0][:], ACT.Tanh, scale=0.5)
         shrink0 = new_tile("shrink0", HALF)
         nc.vector.scalar_tensor_tensor(shrink0[:], tanh0[:], 1.0, va[:, halves[0]], ALU.subtract, ALU.mult)
-        for q in range(4):
-            picked_mean = mean_sb[:].indirect(entries(track_sb, q * PIECE, (q + 1) * PIECE))
-            if q == 0:
-                nc.vector.tensor_copy(mu[q][:], picked_mean)
-            else:
-                nc.scalar.activation(mu[q][:], picked_mean, ACT.Copy)
+        for lo, hi in ((0,128,),(128,192,),):
+            nc.vector.tensor_copy(mu[:, lo:hi], mean_sb[:].indirect(entries(track_sb, lo, hi)))
+        for lo, hi in ((192,256,),(256,384,),(384,512,),):
+            nc.scalar.activation(mu[:, lo:hi], mean_sb[:].indirect(entries(track_sb, lo, hi)), ACT.Copy)
         tanh1 = new_tile("tanh1", HALF)
         nc.scalar.activation(tanh1[:], logit[1][:], ACT.Tanh, scale=0.5)
         tanh = [(tanh0, tanh1)[q // 2][:, quarters[q % 2]] for q in range(4)]
         for q in range(4):
-            nc.vector.tensor_tensor(resid[q][:], y_ps[q][:], mu[q][:], ALU.subtract)
+            nc.vector.tensor_tensor(resid[q][:], y_ps[q][:], mu[:, quarters[q]], ALU.subtract)
         for q in range(4):
             nc.vector.scalar_tensor_tensor(corr[q][:], tanh[q], 1.0, resid[q][:], ALU.add, ALU.mult)
             nc.scalar.activation(widen[q][:], corr[q][:], ACT.Square, scale=math.sqrt(0.1) / 2)

@@ -77,9 +77,12 @@ def tile_picked_ykal_var_p_kernel(
         ln_var = late.tile([P, U], F32, name="ln_var", offset=1024)
         ln_va = new_tile("ln_va", S)
         va = new_tile("va", S)
-        nc.scalar.activation(ln_var[:], var_sb[:], ACT.Ln)
-        nc.scalar.activation(ln_va[:], ln_var[:].indirect(track_sb[:]), ACT.Copy)
-        nc.scalar.activation(va[:], ln_va[:], ACT.Exp)
+        for lo in (0, U // 2):
+            nc.scalar.activation(ln_var[:, lo : lo + U // 2], var_sb[:, lo : lo + U // 2], ACT.Ln)
+        for lo in (0, HALF):
+            nc.scalar.activation(ln_va[:, lo : lo + HALF], ln_var[:].indirect(entries(track_sb, lo, lo + HALF)), ACT.Copy)
+        for lo in (0, HALF):
+            nc.scalar.activation(va[:, lo : lo + HALF], ln_va[:, lo : lo + HALF], ACT.Exp)
 
         def quantize(grouped, name, width):
             codes = new_tile(name + "_codes", width, U32, align_bytes=64)

@@ -79,8 +79,7 @@ def tile_picked_ykal_var_p_kernel(
         va = new_tile("va", S)
         for lo in (0, U // 2):
             nc.scalar.activation(ln_var[:, lo : lo + U // 2], var_sb[:, lo : lo + U // 2], ACT.Ln)
-        for lo in (0, HALF):
-            nc.scalar.activation(ln_va[:, lo : lo + HALF], ln_var[:].indirect(entries(track_sb, lo, lo + HALF)), ACT.Copy)
+        nc.scalar.activation(ln_va[:], ln_var[:].indirect(track_sb[:]), ACT.Copy)
         for lo in (0, HALF):
             nc.scalar.activation(va[:, lo : lo + HALF], ln_va[:, lo : lo + HALF], ACT.Exp)
 

from contextlib import ExitStack
import math

import concourse.mybir as mybir

K, T, S, N, U = 1024, 2048, 512, 128, 1024
FLOPS = 2 * 2 * K * N * S

F32 = mybir.dt.float32
BF16 = mybir.dt.bfloat16
I32 = mybir.dt.int32
U32 = mybir.dt.uint32
U16 = mybir.dt.uint16
U8 = mybir.dt.uint8
FP8X4 = mybir.dt.float8_e4m3fn_x4
ALU = mybir.AluOpType
ACT = mybir.ActivationFunctionType

P = 128
PACK = 4
K_PASS = P * PACK
PASSES = K // K_PASS
QUADRANT = 32
PLANE_ROWS = 4
LIST_ROWS = 16
RUN = 4
HALF = S // 2
PIECE = S // 4
ON_GPSIMD = 32
ON_VECTOR = 48


def tile_picked_ykal_var_p_kernel(
    tc, x_words, x_scales, mean, var, w1, w2, offs, track, out
):
    nc = tc.nc
    with ExitStack() as ctx:
        pool = ctx.enter_context(tc.tile_pool(name="keep", bufs=1))
        late = ctx.enter_context(tc.tile_pool(name="late", bufs=1))
        psum = ctx.enter_context(tc.psum_pool(name="psum", bufs=1))

        def new_tile(name, width, dtype=F32, **options):
            return pool.tile([P, width], dtype, name=name, **options)

        def entries(list_sb, lo, hi):
            return list_sb[:, lo // LIST_ROWS : hi // LIST_ROWS]

        offs_sb = new_tile("offs_sb", S // LIST_ROWS, U16)
        track_sb = new_tile("track_sb", S // LIST_ROWS, U16)
        var_sb = new_tile("var_sb", U, align_bytes=256)
        words = [new_tile(f"words{o}", T, I32, align_bytes=256) for o in range(PASSES)]
        scales = pool.tile([P, PASSES, T], U8, name="scales", align_bytes=256)
        planes = pool.tile([P, PASSES, S], U8, name="planes", align_bytes=256)
        w2_raw = pool.tile([P, PASSES, PACK, N], F32, name="w2_raw", align_bytes=256)

        nc.vector.memset(scales[:].rearrange("p o t -> p (o t)").bitcast(I32), 0)

        nc.sync.dma_start(var_sb[:], var)
        nc.sync.dma_start(track_sb[:], track)
        nc.sync.dma_start(offs_sb[:], offs)
        nc.sync.dma_start(scales[0:P:8, :, :].bitcast(I32), x_scales.rearrange("o r t -> r o t").bitcast(I32))
        nc.sync.dma_start(w2_raw[:], w2.rearrange("(o p j) n -> p o j n", o=PASSES, j=PACK))
        for o in range(PASSES):
            nc.sync.dma_start(words[o][:], x_words[o].rearrange("p t b -> p (t b)").bitcast(I32))

        picked_scales = pool.tile([P, PASSES, S], U8, name="picked_scales", align_bytes=256)
        for o in range(PASSES):
            nc.vector.tensor_copy(picked_scales[:, o, :], scales[:, o, :].indirect(offs_sb[:]))
        nc.vector.tensor_copy(
            planes[:].rearrange("p o s -> p (o s)").bitcast(I32), picked_scales[:].rearrange("p o s -> p (o s)").bitcast(I32)
        )
        for j in range(1, PLANE_ROWS):
            nc.sync.dma_start(
                planes[j:P:QUADRANT].rearrange("p o s -> p (o s)").bitcast(I32),
                picked_scales[8 * j : P : QUADRANT].rearrange("p o s -> p (o s)").bitcast(I32),
            )
        ln_var = late.tile([P, U], F32, name="ln_var", offset=1024)
        ln_va = new_tile("ln_va", S)
        va = new_tile("va", S)
        for lo in (0, U // 2):
            nc.scalar.activation(ln_var[:, lo : lo + U // 2], var_sb[:, lo : lo + U // 2], ACT.Ln)
        nc.scalar.activation(ln_va[:], ln_var[:].indirect(track_sb[:]), ACT.Copy)
        for lo in (0, HALF):
            nc.scalar.activation(va[:, lo : lo + HALF], ln_va[:, lo : lo + HALF], ACT.Exp)

        def quantize(grouped, name, width):
            codes = new_tile(name + "_codes", width, U32, align_bytes=64)
            plane = new_tile(name + "_plane", width, U8, align_bytes=64)
            nc.vector.quantize_mx(out=codes[:].bitcast(FP8X4), scales=plane[:], in_=grouped[:])
            return codes, plane

        w2_bf = new_tile("w2_bf", PASSES * N * PACK, BF16, align_bytes=64)
        nc.vector.tensor_copy(
            w2_bf[:].rearrange("p (o c i j) -> p o c j i", o=PASSES, i=RUN, j=PACK),
            w2_raw[:].rearrange("p o j (c i) -> p o c j i", i=RUN),
        )
        w1_raw = [late.tile([P, PACK, N], F32, name=f"w1_raw{o}", offset=2048 * o) for o in range(PASSES)]
        mean_sb = late.tile([P, U], F32, name="mean_sb", offset=4096)
        for o in range(PASSES):
            nc.sync.dma_start(w1_raw[o][:], w1[K_PASS * o : K_PASS * (o + 1), :].rearrange("(p j) n -> p j n", j=PACK))
        nc.sync.dma_start(mean_sb[:], mean)

        w2_codes, w2_plane = quantize(w2_bf, "w2", PASSES * N)
        w2_mx = [(w2_codes[:, N * o : N * (o + 1)], w2_plane[:, N * o : N * (o + 1)]) for o in range(PASSES)]

        picked_words = [new_tile(f"picked_words{o}", S, U32, align_bytes=64) for o in range(PASSES)]
        z_cols = [slice(0, HALF), slice(HALF, HALF + PIECE), slice(HALF + PIECE, S)]
        quarters = [slice(q * PIECE, (q + 1) * PIECE) for q in range(4)]
        halves = [slice(h * HALF, (h + 1) * HALF) for h in range(2)]
        z_ps = [psum.tile([P, cols.stop - cols.start], F32, name=f"z_ps{i}") for i, cols in enumerate(z_cols)]
        y_ps = [psum.tile([P, PIECE], F32, name=f"y_ps{q}") for q in range(4)]

        def product(acc, weight, o, cols):
            codes, plane = weight
            nc.tensor.matmul_mx(
                out=acc[:],
                lhsT=codes.bitcast(FP8X4),
                lhsT_scale=plane,
                rhs=picked_words[o][:, cols].bitcast(FP8X4),
                rhs_scale=planes[:, o, cols],
                start=(o == 0),
                stop=(o == PASSES - 1),
            )

        nc.vector.tensor_copy(picked_words[0][:], words[0][:].bitcast(U32).indirect(offs_sb[:]))
        for cols in z_cols:
            nc.vector.tensor_copy(
                picked_words[1][:, cols], words[1][:].bitcast(U32).indirect(entries(offs_sb, cols.start, cols.stop))
            )
        for pieces in ([0], [1, 2]):
            for o in range(PASSES):
                for i in pieces:
                    product(z_ps[i], w2_mx[o], o, z_cols[i])

        def rounding_views(o, grouped, lo, hi):
            return (
                grouped[:, PACK * lo : PACK * hi].rearrange("p (c i j) -> p c j i", i=RUN, j=PACK),
                w1_raw[o][:, :, lo:hi].rearrange("p j (c i) -> p c j i", i=RUN),
            )

        w1_bf = [new_tile(f"w1_bf{o}", N * PACK, BF16, align_bytes=64) for o in range(PASSES)]
        nc.scalar.copy(*rounding_views(0, w1_bf[0], 0, N - ON_GPSIMD))
        nc.gpsimd.tensor_scalar(*rounding_views(0, w1_bf[0], N - ON_GPSIMD, N), 1.0, 0.0, ALU.mult, ALU.add)
        nc.scalar.copy(*rounding_views(1, w1_bf[1], 0, N - ON_VECTOR))
        nc.vector.tensor_copy(*rounding_views(1, w1_bf[1], N - ON_VECTOR, N))
        logit = [late.tile([P, HALF], F32, name=f"logit{h}", offset=2048 * h) for h in range(2)]
        tanh0 = late.tile([P, HALF], F32, name="tanh0", offset=3072)
        w1_mx = []
        for o in range(PASSES):
            codes, plane = quantize(w1_bf[o], f"w1_{o}", N)
            w1_mx.append((codes[:], plane[:]))
            if o == 0:
                nc.vector.tensor_tensor(logit[0][:], ln_va[:, z_cols[0]], z_ps[0][:], ALU.subtract)
        nc.vector.tensor_tensor(logit[1][:, :PIECE], ln_va[:, z_cols[1]], z_ps[1][:], ALU.subtract)
        nc.vector.tensor_tensor(logit[1][:, PIECE:], ln_va[:, z_cols[2]], z_ps[2][:], ALU.subtract)
        for o in range(PASSES):
            for q in range(4):
                product(y_ps[q], w1_mx[o], o, quarters[q])

        mu = new_tile("mu", S)
        resid = [new_tile(f"resid{q}", PIECE) for q in range(4)]
        corr = [new_tile(f"corr{q}", PIECE) for q in range(4)]
        widen = [new_tile(f"widen{q}", PIECE) for q in range(4)]
        result = [new_tile(f"result{h}", HALF, align_bytes=256) for h in range(2)]

        nc.scalar.activation(tanh0[:], logit[0][:], ACT.Tanh, scale=0.5)
        shrink0 = new_tile("shrink0", HALF)
        nc.vector.scalar_tensor_tensor(shrink0[:], tanh0[:], 1.0, va[:, halves[0]], ALU.subtract, ALU.mult)
        for lo, hi in ((0,128,),(128,192,),):
            nc.vector.tensor_copy(mu[:, lo:hi], mean_sb[:].indirect(entries(track_sb, lo, hi)))
        for lo, hi in ((192,256,),(256,384,),(384,512,),):
            nc.scalar.activation(mu[:, lo:hi], mean_sb[:].indirect(entries(track_sb, lo, hi)), ACT.Copy)
        tanh1 = new_tile("tanh1", HALF)
        nc.scalar.activation(tanh1[:], logit[1][:], ACT.Tanh, scale=0.5)
        tanh = [(tanh0, tanh1)[q // 2][:, quarters[q % 2]] for q in range(4)]
        for q in range(4):
            nc.vector.tensor_tensor(resid[q][:], y_ps[q][:], mu[:, quarters[q]], ALU.subtract)
        for q in range(4):
            nc.vector.scalar_tensor_tensor(corr[q][:], tanh[q], 1.0, resid[q][:], ALU.add, ALU.mult)
            nc.scalar.activation(widen[q][:], corr[q][:], ACT.Square, scale=math.sqrt(0.1) / 2)
        shrink = [shrink0[:, quarters[0]], shrink0[:, quarters[1]]]
        for q in (2, 3):
            kept = new_tile(f"shrink{q}", PIECE)
            nc.vector.scalar_tensor_tensor(kept[:], tanh[q], 1.0, va[:, quarters[q]], ALU.subtract, ALU.mult)
            shrink.append(kept[:])
        for q in range(4):
            nc.vector.scalar_tensor_tensor(
                result[q // 2][:, quarters[q % 2]], shrink[q], -0.5, widen[q][:], ALU.mult, ALU.add
            )
            if q % 2 == 1:
                nc.sync.dma_start(out[:, halves[q // 2]], result[q // 2][:])
